import numpy as np, ml_dtypes
CORES = [16,32,48,64,80]
N = 5
import mx_ref
BF = ml_dtypes.bfloat16
def entries(a):
    return np.ascontiguousarray(a.T).reshape(-1)
def table(e):
    return np.ascontiguousarray(np.reshape(e, (-1, 16)).T).astype(np.int32)
def cols(t, e):
    v = np.concatenate([t.reshape(128, -1, 4), np.zeros((128, 1, 4), BF)], axis=1)
    return np.ascontiguousarray(v[:, e]).reshape(128, -1)
def cut(t, i, w=512):
    return t[:, w * i:w * i + w]
def f(rng, *shape):
    return mx_ref.flush((rng.standard_normal(shape, dtype=np.float32) * np.exp2(rng.integers(-2, 3, shape[:-1] + (1,)))).astype(BF))
def wide(rng, *shape, cols=0):
    v = rng.standard_normal(shape, dtype=np.float32) * np.exp2(rng.integers(-12, 13, shape)).astype(np.float32)
    if cols: v *= np.repeat(np.exp2(rng.integers(-cols, cols + 1, shape[:-2] + (1, shape[-1] // 4))) * (rng.random(shape[:-2] + (1, shape[-1] // 4)) > 0.0625), 4, axis=-1).astype(np.float32)
    return mx_ref.flush(v.astype(BF))
T, O = 384, 2
def places(rng, dest):
    e = np.zeros((N, T), int)
    for d in range(N): e[dest == d] = d * T + rng.permutation(T)
    return np.stack([table(e[r]) for r in range(N)])
def relabel(rng):
    p = rng.permutation(N)
    if np.all((p - np.arange(N)) % N == p[0]): p[[0, 1]] = p[[1, 0]]
    return p
def setup_inputs(rng):
    e = rng.permutation(N * T).reshape(N, T)
    return {"x": f(rng, N, 128, 4 * T), "to": np.stack([table(e[r]) for r in range(N)]), "w": f(rng, N, 128, 512 * O)}
def setup_inputs_swap(rng):
    d = setup_inputs(rng); p = rng.permutation(N); dest = np.zeros((N, T), int)
    for k in range(N): dest[p[k]] = p[(k + 1) % N]
    d["to"] = places(rng, dest); return d
def setup_inputs_ones(rng):
    d = setup_inputs(rng); i = np.arange(N); n = np.ones((N, N), int); n[i, rng.permutation(N)] += T % N
    for t in range(T // N - 1): n[i, rng.permutation(N)] += N
    d["to"] = places(rng, np.stack([rng.permutation(np.repeat(i, n[r])) for r in range(N)])); return d
def setup_inputs_runs(rng):
    d = setup_inputs(rng); p = relabel(rng); s, u = rng.integers(1, N), rng.integers(0, N); g, h = rng.permutation(N), rng.permutation(N)
    n = T // N + ((g[:, None] + h) % N < T % N)
    j = (np.arange(N) + s * np.arange(N)[:, None] + u) % N
    d["to"] = places(rng, np.stack([np.repeat(p[j[r]], n[r, j[r]]) for r in range(N)])); return d
def setup_inputs_comb(rng):
    d = setup_inputs(rng); p = relabel(rng); s, u = rng.integers(1, N), rng.integers(0, N); k = rng.permutation(N); c = np.arange(T)
    d["to"] = places(rng, np.stack([p[(c + np.where(c < T - T % N, s * r + u, k[r])) % N] for r in range(N)])); return d
def setup_inputs_spread(rng):
    d = setup_inputs(rng); d["x"] = wide(rng, N, 128, 4 * T, cols=8); return d
def check_inputs(d):
    e = np.concatenate([entries(d["to"][r]) for r in range(N)])
    return [] if np.array_equal(np.sort(e), np.arange(N * T)) else ["to"]
def reference(x, to, w):
    z = np.concatenate([x[r] for r in range(N)], axis=1)
    e = np.concatenate([entries(to[r]) for r in range(N)])
    home = np.zeros(N * T, int); home[e] = np.arange(N * T)
    y = np.zeros((N, 128, O * T), np.float32)
    for d in range(N):
        v = mx_ref.quantize(cols(z, home[d * T:d * T + T]))
        for o in range(O): y[d][:, T * o:T * o + T] = mx_ref.matmul(mx_ref.quantize(np.ascontiguousarray(cut(w[d], o))), v)
    return {"y": y}

@@ -1,0 +1,362 @@
+from concourse.bass import DstId, RemoteDMATransfer
+from concourse.mybir import dt, AluOpType, ActivationFunctionType
+
+N, COLS = 5, 384
+SLOT = 80
+SENT1 = 78
+H = 6
+W = COLS // H
+STEP = 1024.0
+
+F32, BF, I32, U16 = "float32", "bfloat16", "int32", "uint16"
+X4, U8 = "float8_e4m3fn_x4", "uint8"
+SMALL = {
+    X4: "q:128,384 wq:128,256 q2:128,400 ql:128,400 q3:128,400 qm:128,400 q4:128,384",
+    U8: "p:128,384 wp:128,256 p2:128,400 pl:128,400 p3:128,400 pm:128,400 p4:128,384",
+    BF: "xt:128,1536 wt:128,1024 nat:128,6,64 val1:128,192 win1:128,400 dup1:128,25,32 tr1:128,800 v3:32,64 val3:128,320 "
+        "win3:128,1920 dup3:128,24,32 tr3:128,768 cs2:128,50",
+    I32: "l0:16,24 e1:32,64 ci2:128,25 pp3:32,64 qq3:32,64",
+    U16: "of1:128,12 l1:128,26 l2:128,26 of3:128,20 l3:128,24",
+    F32: "ys:128,768 lf:16,24 lo_r:32,35 key_r:32,35 thr_r:32,35 run_r:32,35 q_r:128,32 lo_c:32,32 key_c:32,32 thr_c:32,32 "
+         "run_c:32,32 q_c:128,32 ones:128,144 rst:128,125 rst6:32,144 rst2:128,50 tc0:128,5 tcw:128,5 tcb:128,5 lm:32,32 sa0:32,30 "
+         "sam:32,30 lsa:32,30 lst:32,30 mr0:32,5 mr:32,5 mx:32,5 ab0:32,96 ab1:32,96 c1:32,64 ln1:32,32 g1:32,96 z1:32,64 zt1:32,64 "
+         "s1:32,60 sm1:128,25 e2:32,384 jk2:32,384 sg2:32,1 bm2:128,32 row2:128,32 nn2:128,25 o2:128,50 off2:128,25 gx2:128,125 "
+         "fx2:128,125 ss2:128,125 e3:32,64 u3:32,64 na3:32,1 la3:32,32 aa3:32,96 bb3:32,96 g3:32,96 gv3:32,64 xo3:32,10 jk3:32,16 "
+         "cp3:32,1 cv3:32,1 tp3:32,64 ts3:32,64 t3:128,32 tr0:128,32 su3:32,144 sv3:32,144",
+}
+SCRATCH = {"ps": ("psum", [128, 2048], F32), "lists": ("dram", [N, 128, 3], F32)}
+for _t in SMALL:
+    for _b in SMALL[_t].split():
+        SCRATCH[_b.split(":")[0]] = ("sbuf", [int(_n) for _n in _b.split(":")[1].split(",")], _t)
+SEMAPHORES = ["v", "w", "ac", "ap", "ga", "gb", "gn", "ge", "gd", "d_e1", "d_x", "d_w", "d_l", "d_lf", "d_e2", "d_e3", "d_t3",
+              "d_o1", "d_v1", "d_v3", "d_o2", "sl", "s1c", "s1p", "s2c", "s2p", "loc", "m0", "m1", "m2", "m3", "st", "st2"]
+
+
+def rank_program(g, core, T, topo):
+    me = T.rank_of(core)
+    if me is None:
+        return
+    S, V, A = T.sem, g.vector, g.scalar
+    op, FN = AluOpType, ActivationFunctionType
+    COPY, LINE = FN.Copy, FN.Identity
+    others = [r for r in range(N) if r != me]
+    cnt = {"v": 0, "w": 0, "ac": 0, "ga": 0, "gb": 0, "gn": 0, "ge": 0, "gd": 0}
+    CALL = {"ts": V.tensor_scalar, "tt": V.tensor_tensor, "cp": V.tensor_copy, "ms": V.memset,
+            "scan": V.tensor_tensor_scan, "tr": V.transpose, "qz": V.quantize_mx}
+
+    def vec(line, free, name, args):
+        if cnt[line] and not free:
+            V.wait_ge(S[line], cnt[line])
+        if name == "ts":
+            out, a, s1, o1 = args[:4]
+            args = (out, a, s1, None, o1) if len(args) == 4 else (out, a, s1, args[4], o1, args[5])
+        CALL[name](*args).then_inc(S[line], 1)
+        cnt[line] += 1
+        return cnt[line]
+    v = lambda name, *args: vec("v", False, name, args)
+    vf = lambda name, *args: vec("v", True, name, args)
+    w = lambda name, *args: vec("w", False, name, args)
+    wf = lambda name, *args: vec("w", True, name, args)
+
+    def act(out, in_, func, **k):
+        A.activation(out, in_, func, **k).then_inc(S.ac, 1)
+        cnt["ac"] += 1
+        return cnt["ac"]
+
+    def iota(line, out, pattern, base=0, cm=0):
+        g.iota(out, pattern, base, cm, allow_small_or_imprecise_dtypes=True).then_inc(S[line], 1)
+        cnt[line] += 1
+
+    def sel(line, out, in_, pattern, how, base, cm):
+        g.affine_select(out, in_, pattern, how, 0.0, base, cm).then_inc(S[line], 1)
+        cnt[line] += 1
+    R = slice(0, 30)
+
+    g.sync.dma_start(T.l0[:], T.to[:]).then_inc(S.d_l, 16)
+    for d in range(N):
+        (g.sync if d % 2 else A).dma_start(T.e1[d:N * H:N, :], T.to[:]).then_inc(S.d_e1, 16)
+    g.sync.dma_start(T.xt[:, 0:768], T.x[:, 0:768]).then_inc(S.d_x, 16)
+    A.dma_start(T.xt[:, 768:1536], T.x[:, 768:1536]).then_inc(S.d_x, 16)
+    A.dma_start(T.wt[:], T.w[:]).then_inc(S.d_w, 16)
+
+    iota("ga", T.lo_r[:], [[0, H + 1], [COLS, N]])
+    iota("ga", T.key_r[:], [[1, H + 1], [H, N]])
+    nones = vf("ms", T.ones[:], 1.0)
+    for b in ("z1", "ln1"):
+        vf("ms", T[b][:], 0.0)
+    vf("ms", T.ab1[:, 0:32], 0.0)
+    vf("ms", T.val1[:], 0.0)
+    V.wait_ge(S.ga, cnt["ga"])
+    vf("tr", T.lo_c[:], T.lo_r[:, 0:32])
+    vf("tr", T.key_c[:], T.key_r[:, 0:32])
+    v("ts", T.lm[R, :], T.key_r[R, 0:32], T.key_c[R, 0:1], op.is_gt)
+    wf("ms", T.val3[:], 0.0)
+    iota("gn", T.nat[:], [[1, 16], [16, 24]], -192)
+    g.wait_ge(S.v, nones)
+    sel("gb", T.rst[:], T.ones[:, 0:125], [[0, 25], [1, 5]], op.is_gt, 0, 0)
+
+    V.wait_ge(S.d_e1, 80)
+    v("ts", T.ab0[R, 32:96], T.e1[R, :], T.lo_c[R, 0:1], op.is_ge)
+    nab = vf("ts", T.ab1[R, 32:96], T.e1[R, :], -float(COLS), op.add, T.lo_c[R, 0:1], op.is_ge)
+    V.wait_ge(S.d_l, 16)
+    nlf = wf("cp", T.lf[:], T.l0[:])
+    g.sync.wait_ge(S.w, nlf)
+    g.sync.dma_start(T.lists[me], T.lf[:]).then_inc(S.d_lf, 16)
+    g.sync.wait_ge(S.v, nab)
+    g.sync.wait_ge(S.gn, cnt["gn"])
+    for blk in range(2):
+        for odd in range(2):
+            g.sync.dma_start(T.val1[16 * odd:128:32, 96 * blk:96 * blk + 96],
+                             T.nat[16 * odd:128:32, :, 32 * blk + 16 * odd:32 * blk + 16 * odd + 16]).then_inc(S.d_v1, 16)
+
+    per = len(topo.engines(core, T.cores[others[0]])) // len(others)
+    landed = per * len(others)
+
+    def spread(src, dst, sem):
+        moves = []
+        for i, r in enumerate(others):
+            rid, pid, _ = topo.addr(T.cores[r])
+            e = topo.engines(core, T.cores[r])[per * i:per * i + per]
+            moves.append(RemoteDMATransfer(dst_ids=[DstId(rid=rid, pnc=pid)], dma_engine_mask=sum(1 << b for b in e),
+                                           remote_sem=sem, srcs=[src(r)], dsts=[dst]))
+        g.remote_dma_fused(moves, local_sem=S.loc)
+
+    iota("ge", T.thr_r[:], [[-2 * COLS, H + 1], [0, N]], 1)
+    iota("ge", T.run_r[:], [[0, H + 1], [-10 * SLOT, N]])
+    iota("ge", T.q_r[:], [[0, 2], [1, 16]])
+    iota("ge", T.tc0[:], [[16, 5]])
+    g.wait_ge(S.d_lf, 16)
+    spread(lambda r: T.lists[me], T.lists[me], S.sl)
+
+    sel("gd", T.sa0[:], T.ones[0:32, 0:30], [[-H, 5], [0, H]], op.is_ge, 0, 1)
+    sel("gd", T.mr0[:], T.ones[0:32, 0:5], [[-H, 5]], op.is_ge, 0, 1)
+    sel("gd", T.rst2[:], T.ones[:, 0:50], [[0, 5], [1, 10]], op.not_equal, -1, 0)
+    g.wait_ge(S.gd, cnt["gd"])
+    sel("gd", T.sam[:], T.sa0[:], [[H, 5], [0, H]], op.is_ge, H - 1, -1)
+    sel("gd", T.mr[:], T.mr0[:], [[H, 5]], op.is_ge, H - 1, -1)
+    g.wait_ge(S.gd, cnt["gd"])
+    sel("gd", T.lsa[:], T.sam[:], [[1, 30]], op.is_gt, 0, -1)
+    sel("gd", T.lst[:], T.sam[:], [[-1, 30]], op.is_gt, 0, 1)
+    sel("gd", T.rst6[:], T.ones[0:32, :], [[0, 24], [1, H]], op.is_gt, 0, 0)
+
+    v("scan", T.c1[R, :], T.ab0[R, 32:96], T.ab1[R, 32:96], 0.0, op.add, op.subtract)
+    wf("ms", T.win1[:, 0:200], 0.0)
+    v("ts", T.ln1[R, :], T.lm[R, :], T.c1[R, W - 1:W], op.mult)
+    wf("ms", T.win1[:, 200:400], 0.0)
+    v("tr", T.ab0[:, 0:32], T.ln1[:])
+    for b in ("t3", "bm2", "la3"):
+        wf("ms", T[b][:], 0.0)
+    nz = cnt["w"]
+    v("scan", T.g1[R, :], T.ab0[R, :], T.ab1[R, :], 0.0, op.add, op.subtract)
+
+    def pack(b):
+        return wf("qz", T.q[:, 128 * b:128 * b + 128], T.p[:, 128 * b:128 * b + 128], T.xt[:, 512 * b:512 * b + 512])
+    V.wait_ge(S.d_x, 32)
+    pack(0)
+    v("tt", T.z1[R, :], T.g1[R, 32:96], T.ab0[R, 32:96], op.mult)
+    pack(1)
+    v("tr", T.zt1[:], T.z1[:])
+    n1 = pack(2)
+    V.wait_ge(S.gb, cnt["gb"])
+    v("scan", T.s1[:, 0:30], T.rst[0:32, 0:30], T.zt1[:, 0:30], 0.0, op.mult, op.max)
+    vf("scan", T.s1[:, 30:60], T.rst[0:32, 0:30], T.zt1[:, 32:62], 0.0, op.mult, op.max)
+    wf("ms", T.cs2[:], -128.0)
+    v("ts", T.of1[0:32, :], T.s1[:, 4:60:5], -1.0, op.add)
+    for a in range(1, 4):
+        vf("ts", T.of1[32 * a:32 * a + 32, :], T.s1[:, 4:60:5], -1.0, op.add)
+    V.wait_ge(S.w, n1)
+    V.wait_ge(S.d_v1, 64)
+    nw1 = v("cp", T.win1[:, 0:400].indirect(T.of1[:, 0:12]), T.val1[:])
+    A.wait_ge(S.v, nw1)
+    V.wait_ge(S.ge, cnt["ge"])
+    nct = wf("tr", T.thr_c[:], T.thr_r[:, 0:32])
+    V.wait_ge(S.v, nw1)
+    for k in range(N):
+        for u in (0, 16):
+            out, in_ = T.dup1[:, 5 * k:5 * k + 5, u:u + 16], T.win1[:, k:400:5]
+            if k < 3:
+                vf("cp", out, in_)
+            else:
+                nd1 = act(out, in_, COPY)
+    V.wait_ge(S.ac, nd1)
+    v("tr", T.tr1[:], T.dup1[:])
+    wf("tr", T.q_c[:], T.q_r[:])
+    nrc = wf("tr", T.run_c[:], T.run_r[:, 0:32])
+    v("tt", T.sm1[:], T.tr1[:, 0:800:32], T.tr1[:, 16:800:32], op.add)
+    w("ts", T.tcw[:], T.tc0[:], T.q_c[:, 0:1], op.add)
+    nl1 = v("ts", T.l1[:, 0:25], T.sm1[:], 192.0, op.add)
+    w("ts", T.tcb[:], T.tcw[:], 0.5, op.add, STEP, op.mult)
+    k1 = v("cp", T.q2[:].bitcast(dt.uint32), T.q[:].bitcast(dt.uint32).indirect(T.l1[:, 0:25]))
+    A.wait_ge(S.w, n1)
+    A.wait_ge(S.v, nl1)
+    A.activation(T.p2[:], T.p[:].indirect(T.l1[:, 0:25]), COPY).then_inc(S.ap, 1)
+
+    cut = lambda r, n: slice(SLOT * r, SLOT * r + n)
+    g.wait_ge(S.v, k1)
+    spread(lambda r: T.q2[:, cut(r, SENT1)].bitcast(dt.uint8), T.ql[:, cut(me, SENT1)].bitcast(dt.uint8), S.s1c)
+    g.wait_ge(S.ap, 1)
+    spread(lambda r: T.p2[:, cut(r, SENT1)], T.pl[:, cut(me, SENT1)], S.s1p)
+
+    g.sync.wait_ge(S.w, nz)
+    g.sync.wait_ge(S.sl, landed)
+    g.sync.wait_ge(S.d_lf, 16)
+    for d in range(N + 1):
+        g.sync.dma_start(T.e2[N * d:N * d + N, :], T.lists[:]).then_inc(S.d_e2, 16)
+    g.sync.dma_start(T.e3[R, :], T.lists[:]).then_inc(S.d_e3, 16)
+    g.sync.wait_ge(S.d_e3, 16)
+    for b in range(8):
+        g.sync.dma_start(T.t3[32 * (b // 2):32 * (b // 2) + 20, 16 * (b % 2):16 * (b % 2) + 16],
+                         T.e3[5 * (b % H):5 * (b % H) + 5, :]).then_inc(S.d_t3, 16)
+    g.sync.wait_ge(S.v, k1)
+    g.sync.dma_start(T.ql[:, cut(me, SLOT)].bitcast(dt.uint8), T.q2[:, cut(me, SLOT)].bitcast(dt.uint8)).then_inc(S.d_o1, 16)
+    g.sync.wait_ge(S.ap, 1)
+    g.sync.dma_start(T.pl[:, cut(me, SLOT)], T.p2[:, cut(me, SLOT)]).then_inc(S.d_o1, 16)
+
+    A.wait_ge(S.d_e2, 96)
+    A.wait_ge(S.w, nct)
+    nsg = act(T.jk2[R, :], T.e2[R, :], FN.Sign, scale=2.0, bias=T.thr_c[R, 0:1], accum_out=T.sg2[R, 0:1])
+    A.wait_ge(S.d_e3, 16)
+    nu3 = act(T.u3[R, :], T.e3[R, :], FN.Abs, scale=2.0, bias=-float(2 * COLS * me + COLS - 1))
+    A.wait_ge(S.ac, nsg)
+    A.wait_ge(S.w, nrc)
+    for a in range(2):
+        nbm = act(T.bm2[32 * a:32 * a + 30, :], T.ones[R, 0:32], LINE, scale=T.sg2[R, 0:1], bias=T.run_c[R, 0:1])
+    A.wait_ge(S.ac, nu3)
+    ni3 = act(T.aa3[R, 32:96], T.u3[R, :], FN.Sign, scale=-1.0, bias=float(COLS), accum_out=T.na3[R, 0:1])
+    A.wait_ge(S.gd, cnt["gd"])
+    A.wait_ge(S.ac, ni3)
+    nla = act(T.la3[R, 0:30], T.lsa[R, :], LINE, scale=T.na3[R, 0:1])
+
+    wf("ms", T.cs2[:, 1:50:10], 0.0)
+    V.wait_ge(S.gd, cnt["gd"])
+    wf("ts", T.bb3[R, 0:30], T.lst[R, :], float(W), op.mult)
+    wf("ms", T.bb3[:, 30:32], 0.0)
+    wf("ms", T.bb3[:, 32:96], 1.0)
+    wf("ts", T.mx[R, :], T.mr[R, :], -40.0, op.mult)
+    V.wait_ge(S.ac, nsg)
+    for a in range(2, 4):
+        vf("ts", T.bm2[32 * a:32 * a + 30, :], T.ones[R, 0:32], T.sg2[R, 0:1], op.mult, T.run_c[R, 0:1], op.add)
+    V.wait_ge(S.ac, nbm)
+    v("tr", T.row2[:], T.bm2[:])
+    v("tt", T.nn2[:], T.row2[:, 0:25], T.row2[:, 5:30], op.subtract)
+    vf("ts", T.ci2[:], T.row2[:, 0:25], -0.1, op.mult, 38.8 - 0.2 * me, op.add)
+    v("ts", T.cs2[:, 2:50:2], T.nn2[:, 0:24], 0.1, op.mult, 128.4, op.add)
+    V.wait_ge(S.ac, nla)
+    wf("tr", T.aa3[:, 0:32], T.la3[:])
+    V.wait_ge(S.w, cnt["w"] - 1)
+    v("scan", T.o2[:], T.rst2[:], T.cs2[:], 0.0, op.mult, op.add)
+    ng3 = w("scan", T.g3[R, :], T.aa3[R, :], T.bb3[R, :], 0.0, op.add, op.add)
+    noff = v("tt", T.off2[:], T.ci2[:], T.o2[:, 1:50:2], op.subtract)
+    vf("tt", T.xo3[R, 0:5], T.row2[R, 5 * me:5 * me + 5], T.mx[R, :], op.mult)
+    nxo = vf("tt", T.xo3[R, 5:10], T.o2[R, 10 * me + 1:10 * me + 10:2], T.mr[R, :], op.mult)
+    nqq = w("ts", T.qq3[R, :], T.g3[R, 32:96], 0.1, op.mult, -0.6, op.add)
+    A.wait_ge(S.w, ng3)
+    ngv = act(T.gv3[R, :], T.g3[R, 32:96], LINE, scale=40.0, bias=15080.0)
+    A.wait_ge(S.v, nxo)
+    ncp = act(T.jk3[R, 0:5], T.xo3[R, 0:5], LINE, scale=0.0025, bias=7.56, accum_out=T.cp3[R, 0:1])
+    ncv = act(T.jk3[R, 5:15], T.xo3[R, :], LINE, accum_out=T.cv3[R, 0:1])
+    for j in range(N):
+        nfx = act(T.fx2[:, 25 * j:25 * j + 25], T.off2[:], LINE, bias=T.tcw[:, j:j + 1])
+    for j in range(N):
+        vf("ts", T.gx2[:, 25 * j:25 * j + 25], T.o2[:, 1:50:2], -STEP, op.mult, T.tcb[:, j:j + 1], op.add)
+    V.wait_ge(S.ac, ncp)
+    npp = wf("ts", T.pp3[R, :], T.g3[R, 32:96], 0.1, op.mult, T.cp3[R, 0:1], op.add)
+    V.wait_ge(S.w, nqq)
+    wf("tt", T.ts3[R, :], T.gv3[R, :], T.qq3[R, :], op.add)
+    V.wait_ge(S.w, npp)
+    V.wait_ge(S.ac, ncv)
+    wf("ts", T.tp3[R, :], T.pp3[R, :], -400.0, op.mult, T.cv3[R, 0:1], op.add)
+    V.wait_ge(S.ac, nfx)
+    v("scan", T.ss2[:], T.gx2[:], T.fx2[:], 0.0, op.max, op.min)
+    nv3 = w("tt", T.v3[R, :], T.tp3[R, :], T.ts3[R, :], op.add)
+    V.wait_ge(S.v, cnt["v"])
+    for j in range(N):
+        n2 = vf("ts", T.l2[:, j:25:5], T.ss2[:, 25 * j + 4:25 * j + 25:5], float(SLOT * (N - 1) + SENT1 - 1), op.min)
+
+    V.wait_ge(S.v, n2)
+    V.wait_ge(S.s1c, landed)
+    V.wait_ge(S.d_o1, 32)
+    k2 = v("cp", T.q3[:].bitcast(dt.uint32), T.ql[:].bitcast(dt.uint32).indirect(T.l2[:, 0:25]))
+    A.wait_ge(S.v, n2)
+    A.wait_ge(S.s1p, landed)
+    A.wait_ge(S.d_o1, 32)
+    A.activation(T.p3[:], T.pl[:].indirect(T.l2[:, 0:25]), COPY).then_inc(S.ap, 1)
+    g.wait_ge(S.v, k2)
+    spread(lambda r: T.q3[:, cut(r, SLOT)].bitcast(dt.uint8), T.qm[:, cut(me, SLOT)].bitcast(dt.uint8), S.s2c)
+    g.wait_ge(S.ap, 2)
+    spread(lambda r: T.p3[:, cut(r, SLOT)], T.pm[:, cut(me, SLOT)], S.s2p)
+    g.sync.wait_ge(S.w, nv3)
+    g.sync.dma_start(T.val3[0:96:16, :], T.v3[R, :]).then_inc(S.d_v3, 16)
+    g.sync.wait_ge(S.v, k2)
+    g.sync.dma_start(T.qm[:, cut(me, SLOT)].bitcast(dt.uint8), T.q3[:, cut(me, SLOT)].bitcast(dt.uint8)).then_inc(S.d_o2, 16)
+    g.sync.wait_ge(S.ap, 2)
+    g.sync.dma_start(T.pm[:, cut(me, SLOT)], T.p3[:, cut(me, SLOT)]).then_inc(S.d_o2, 16)
+
+    V.wait_ge(S.d_t3, 128)
+    nt0 = wf("tr", T.tr0[:], T.t3[:])
+    V.wait_ge(S.d_w, 16)
+    wf("qz", T.wq[:], T.wp[:], T.wt[:])
+    mine = COLS * me
+    wf("ms", T.win3[:, mine:mine + COLS], 0.0)
+    V.wait_ge(S.w, nt0)
+    wf("cp", T.of3[:], T.tr0[:, 0:20])
+    V.wait_ge(S.d_v3, 16)
+    nw3 = w("cp", T.win3[:].indirect(T.of3[:]), T.val3[:])
+    A.wait_ge(S.w, nw3)
+    nd3 = act(T.dup3[:, 12:24, 16:32], T.win3[:, mine + 192:mine + 384], COPY)
+    w("cp", T.dup3[:, :, 0:16], T.win3[:, mine:mine + 384])
+    wf("cp", T.dup3[:, 0:12, 16:32], T.win3[:, mine:mine + 192])
+    V.wait_ge(S.ac, nd3)
+    nt3 = w("tr", T.tr3[:], T.dup3[:])
+    A.wait_ge(S.w, nt3)
+    V.wait_ge(S.w, nt3)
+    for r in range(H):
+        out, in_ = T.su3[:, r:144:6], T.tr3[32 * (r // 2):32 * (r // 2) + 32, 16 * (r % 2):768:32]
+        if r < 3:
+            wf("cp", out, in_)
+        else:
+            nsu = act(out, in_, COPY)
+    V.wait_ge(S.ac, nsu)
+    w("scan", T.sv3[:], T.rst6[:], T.su3[:], 0.0, op.mult, op.add)
+    w("ts", T.l3[0:32, :], T.sv3[:, 5:144:6], 200.0, op.add)
+    for a in range(1, 4):
+        n3 = wf("ts", T.l3[32 * a:32 * a + 32, :], T.sv3[:, 5:144:6], 200.0, op.add)
+
+    V.wait_ge(S.s2c, landed)
+    V.wait_ge(S.d_o2, 32)
+    V.wait_ge(S.w, n3)
+    A.wait_ge(S.w, n3)
+    A.wait_ge(S.s2p, landed)
+    A.wait_ge(S.d_o2, 32)
+    HALF = COLS // 2
+    for h in range(2):
+        c = slice(HALF * h, HALF * h + HALF)
+        off = T.l3[:, 12 * h:12 * h + 12]
+        nk = vf("cp", T.q4[:, c].bitcast(dt.uint32), T.qm[:].bitcast(dt.uint32).indirect(off))
+        A.activation(T.p4[:, c], T.pm[:].indirect(off), COPY).then_inc(S.ap, 1)
+        g.tensor.wait_ge(S.v, nk)
+        g.tensor.wait_ge(S.ap, 3 + h)
+        for o in range(2):
+            b = 2 * h + o
+            g.tensor.matmul_mx(T.ps[:, 512 * b:512 * b + HALF], T.wq[:, 128 * o:128 * o + 128], T.wp[:, 128 * o:128 * o + 128],
+                               T.q4[:, c], T.p4[:, c], True, True).then_inc(S["m%d" % b], 1)
+    for h in range(2):
+        for o in range(2):
+            b = 2 * h + o
+            y = T.ys[:, COLS * o + HALF * h:COLS * o + HALF * h + HALF]
+            out = T.y[:, COLS * o + HALF * h:COLS * o + HALF * h + HALF]
+            if o == 0:
+                V.wait_ge(S["m%d" % b], 1)
+                ny = vf("cp", y, T.ps[:, 512 * b:512 * b + HALF])
+                g.sync.wait_ge(S.v, ny)
+                g.sync.dma_start(out, y).then_inc(S.st, 16)
+            else:
+                A.wait_ge(S["m%d" % b], 1)
+                ny = act(y, T.ps[:, 512 * b:512 * b + HALF], COPY)
+                A.wait_ge(S.ac, ny)
+                A.dma_start(out, y).then_inc(S.st2, 16)
+    g.sync.wait_ge(S.st, 32)
+    A.wait_ge(S.st2, 32)
+    g.wait_ge(S.v, cnt["v"])
+    g.wait_ge(S.w, cnt["w"])
+    g.wait_ge(S.loc, 5 * landed)

@@ -7,356 +7,291 @@ SENT1 = 78
 H = 6
 W = COLS // H
 STEP = 1024.0
+BIG = 512.0
+G = 8
+PER = 4 * W
 
 F32, BF, I32, U16 = "float32", "bfloat16", "int32", "uint16"
 X4, U8 = "float8_e4m3fn_x4", "uint8"
 SMALL = {
-    X4: "q:128,384 wq:128,256 q2:128,400 ql:128,400 q3:128,400 qm:128,400 q4:128,384",
-    U8: "p:128,384 wp:128,256 p2:128,400 pl:128,400 p3:128,400 pm:128,400 p4:128,384",
-    BF: "xt:128,1536 wt:128,1024 nat:128,6,64 val1:128,192 win1:128,400 dup1:128,25,32 tr1:128,800 v3:32,64 val3:128,320 "
-        "win3:128,1920 dup3:128,24,32 tr3:128,768 cs2:128,50",
-    I32: "l0:16,24 e1:32,64 ci2:128,25 pp3:32,64 qq3:32,64",
-    U16: "of1:128,12 l1:128,26 l2:128,26 of3:128,20 l3:128,24",
-    F32: "ys:128,768 lf:16,24 lo_r:32,35 key_r:32,35 thr_r:32,35 run_r:32,35 q_r:128,32 lo_c:32,32 key_c:32,32 thr_c:32,32 "
-         "run_c:32,32 q_c:128,32 ones:128,144 rst:128,125 rst6:32,144 rst2:128,50 tc0:128,5 tcw:128,5 tcb:128,5 lm:32,32 sa0:32,30 "
-         "sam:32,30 lsa:32,30 lst:32,30 mr0:32,5 mr:32,5 mx:32,5 ab0:32,96 ab1:32,96 c1:32,64 ln1:32,32 g1:32,96 z1:32,64 zt1:32,64 "
-         "s1:32,60 sm1:128,25 e2:32,384 jk2:32,384 sg2:32,1 bm2:128,32 row2:128,32 nn2:128,25 o2:128,50 off2:128,25 gx2:128,125 "
-         "fx2:128,125 ss2:128,125 e3:32,64 u3:32,64 na3:32,1 la3:32,32 aa3:32,96 bb3:32,96 g3:32,96 gv3:32,64 xo3:32,10 jk3:32,16 "
-         "cp3:32,1 cv3:32,1 tp3:32,64 ts3:32,64 t3:128,32 tr0:128,32 su3:32,144 sv3:32,144",
+    X4: "q:128,384 wq:128,256 q2:128,320 ql:128,400 q3:128,320 qm:128,400",
+    U8: "p:128,384 wp:128,256 p2:128,320 pl:128,400 p3:128,320 pm:128,400",
+    BF: "xt:128,1536 wt:128,1024 nat:128,6,64 val1:128,192 win1:128,400 dup1:128,25,32 tr1:128,800 bmp:128,32 rowp:128,32 "
+        "land:128,5,8 cs2:128,32 v3:32,64 val3:128,256 win3:128,1920 dup3:128,24,32 tr3:128,768 rst8:32,192 su3:32,192 sv3:32,192",
+    I32: "e1:32,64 ci0:128,25 ci2:128,32 e3:32,64 t3:128,32 pp3:32,64 qq3:32,64",
+    U16: "of1:128,12 l1:128,26 of2:128,8 l2:128,26 of3:128,16 l3:128,24",
+    F32: "ys:128,768 rs0:128,400 rs1:128,400 lo_r:32,35 key_r:32,35 q_r:128,32 lo_c:32,32 key_c:32,32 q_c:128,32 ones:128,192 "
+         "rst:128,130 lm:32,32 ab0:32,64 ab1:32,64 big1:32,65 up1:32,96 dn1:32,96 c1:32,64 ln1:32,32 g1:32,96 zt1:32,64 s1:32,60 "
+         "sm1:128,25 f2:32,128 z2:128,32 zc2:128,32 tb0:128,25 tb2:128,128 t80:128,25 nn2:128,25 d2:128,128 u2:128,128 gx2:128,128 "
+         "fx2:128,128 ss2:128,125 sa0:32,30 sam:32,30 lsa:32,30 c80:32,5 mx0:32,5 mx:32,5 low:32,5 gb3:32,1 ea3:32,96 eb3:32,96 "
+         "c3:32,64 la3:32,32 g3:32,96 gv3:32,64 xo3:32,10 jk3:32,20 cp3:32,1 cv3:32,1 tp3:32,64 ts3:32,64 tf3:128,32 tr0:128,32",
 }
-SCRATCH = {"ps": ("psum", [128, 2048], F32), "lists": ("dram", [N, 128, 3], F32)}
+SCRATCH = {"ps": ("psum", [128, 2048], F32), "lists": ("dram", [N * 128, 3], I32)}
 for _t in SMALL:
     for _b in SMALL[_t].split():
         SCRATCH[_b.split(":")[0]] = ("sbuf", [int(_n) for _n in _b.split(":")[1].split(",")], _t)
-SEMAPHORES = ["v", "w", "ac", "ap", "ga", "gb", "gn", "ge", "gd", "d_e1", "d_x", "d_w", "d_l", "d_lf", "d_e2", "d_e3", "d_t3",
-              "d_o1", "d_v1", "d_v3", "d_o2", "sl", "s1c", "s1p", "s2c", "s2p", "loc", "m0", "m1", "m2", "m3", "st", "st2"]
+SEMAPHORES = ["v", "a", "g", "m", "d_e1", "d_x", "d_w", "d_l", "d_z", "d_e3", "d_t3", "d_v1", "d_v3",
+              "sl", "sp", "s1c", "s1p", "s2c", "s2p", "loc", "st", "st2"]
+
+
+def cut(r, n):
+    return slice(SLOT * r, SLOT * r + n)
 
 
 def rank_program(g, core, T, topo):
     me = T.rank_of(core)
     if me is None:
         return
-    S, V, A = T.sem, g.vector, g.scalar
+    S, V, A, Y = T.sem, g.vector, g.scalar, g.sync
     op, FN = AluOpType, ActivationFunctionType
     COPY, LINE = FN.Copy, FN.Identity
-    others = [r for r in range(N) if r != me]
-    cnt = {"v": 0, "w": 0, "ac": 0, "ga": 0, "gb": 0, "gn": 0, "ge": 0, "gd": 0}
+    order = [(me + 1 + i) % N for i in range(N)]
+    rest = N - 1 - me
+    far = topo.engines(core, T.cores[order[0]])
+    queues = {"v": V, "a": A, "g": g, "y": Y, "m": g.tensor}
+    count, seen = {}, {}
     CALL = {"ts": V.tensor_scalar, "tt": V.tensor_tensor, "cp": V.tensor_copy, "ms": V.memset,
             "scan": V.tensor_tensor_scan, "tr": V.transpose, "qz": V.quantize_mx}
 
-    def vec(line, free, name, args):
-        if cnt[line] and not free:
-            V.wait_ge(S[line], cnt[line])
+    def wait(q, marks):
+        for sem, n in marks:
+            if seen.get((q, sem), 0) < n:
+                queues[q].wait_ge(S[sem], n)
+                seen[q, sem] = n
+
+    def mark(call, sem, n):
+        call.then_inc(S[sem], n)
+        count[sem] = count.get(sem, 0) + n
+        return sem, count[sem]
+
+    def v(name, *args, after=()):
+        wait("v", after)
         if name == "ts":
             out, a, s1, o1 = args[:4]
             args = (out, a, s1, None, o1) if len(args) == 4 else (out, a, s1, args[4], o1, args[5])
-        CALL[name](*args).then_inc(S[line], 1)
-        cnt[line] += 1
-        return cnt[line]
-    v = lambda name, *args: vec("v", False, name, args)
-    vf = lambda name, *args: vec("v", True, name, args)
-    w = lambda name, *args: vec("w", False, name, args)
-    wf = lambda name, *args: vec("w", True, name, args)
+        return mark(CALL[name](*args), "v", 1)
 
-    def act(out, in_, func, **k):
-        A.activation(out, in_, func, **k).then_inc(S.ac, 1)
-        cnt["ac"] += 1
-        return cnt["ac"]
+    def act(out, in_, func, after=(), **k):
+        wait("a", after)
+        return mark(A.activation(out, in_, func, **k), "a", 1)
 
-    def iota(line, out, pattern, base=0, cm=0):
-        g.iota(out, pattern, base, cm, allow_small_or_imprecise_dtypes=True).then_inc(S[line], 1)
-        cnt[line] += 1
+    def fill(buf, rows, c0, c1, value, step=1, after=()):
+        return act(buf[0:rows, c0:c1:step], T.ones[0:rows, 0:(c1 - c0) // step], COPY, scale=value, after=after)
 
-    def sel(line, out, in_, pattern, how, base, cm):
-        g.affine_select(out, in_, pattern, how, 0.0, base, cm).then_inc(S[line], 1)
-        cnt[line] += 1
-    R = slice(0, 30)
+    def iota(out, pattern, base=0, after=()):
+        wait("g", after)
+        return mark(g.iota(out, pattern, base, 0, allow_small_or_imprecise_dtypes=True), "g", 1)
 
-    g.sync.dma_start(T.l0[:], T.to[:]).then_inc(S.d_l, 16)
+    def sel(out, in_, pattern, how, base, cm, after=()):
+        wait("g", after)
+        return mark(g.affine_select(out, in_, pattern, how, 0.0, base, cm), "g", 1)
+
+    def dma(q, out, in_, sem, after=()):
+        wait(q, after)
+        return mark(queues[q].dma_start(out, in_), sem, 16)
+
+    def codes(out, win, off, after=()):
+        return v("cp", out.bitcast(dt.uint32), win[:].bitcast(dt.uint32).indirect(off), after=after)
+
+    def planes(out, win, off, after=()):
+        return act(out, win[:].indirect(off), COPY, after=after)
+
+    def send(moves, sem, after):
+        wait("g", after)
+        per, out = len(far) // len(moves), []
+        for i, (r, src, dst) in enumerate(moves):
+            rid, pid, _ = topo.addr(T.cores[r])
+            out.append(RemoteDMATransfer(dst_ids=[DstId(rid=rid, pnc=pid)], dma_engine_mask=sum(1 << b for b in far[per * i:per * i + per]),
+                                         remote_sem=S[sem], srcs=[src], dsts=[dst]))
+        g.remote_dma_fused(out, local_sem=S.loc)
+        for s in (sem, "loc"):
+            count[s] = count.get(s, 0) + len(far)
+        return sem, count[sem]
+    R = slice(0, N * H)
+    own, mine = T.lists[128 * me:128 * me + 128, :], COLS * me
+
+    l_own = dma("y", own, T.to[:], "d_l")
     for d in range(N):
-        (g.sync if d % 2 else A).dma_start(T.e1[d:N * H:N, :], T.to[:]).then_inc(S.d_e1, 16)
-    g.sync.dma_start(T.xt[:, 0:768], T.x[:, 0:768]).then_inc(S.d_x, 16)
-    A.dma_start(T.xt[:, 768:1536], T.x[:, 768:1536]).then_inc(S.d_x, 16)
-    A.dma_start(T.wt[:], T.w[:]).then_inc(S.d_w, 16)
+        l_e1 = dma("y" if d % 2 else "a", T.e1[d:N * H:N, :], T.to[:], "d_e1")
+    dma("y", T.xt[:, 0:768], T.x[:, 0:768], "d_x")
+    l_x = dma("a", T.xt[:, 768:1536], T.x[:, 768:1536], "d_x")
 
-    iota("ga", T.lo_r[:], [[0, H + 1], [COLS, N]])
-    iota("ga", T.key_r[:], [[1, H + 1], [H, N]])
-    nones = vf("ms", T.ones[:], 1.0)
-    for b in ("z1", "ln1"):
-        vf("ms", T[b][:], 0.0)
-    vf("ms", T.ab1[:, 0:32], 0.0)
-    vf("ms", T.val1[:], 0.0)
-    V.wait_ge(S.ga, cnt["ga"])
-    vf("tr", T.lo_c[:], T.lo_r[:, 0:32])
-    vf("tr", T.key_c[:], T.key_r[:, 0:32])
-    v("ts", T.lm[R, :], T.key_r[R, 0:32], T.key_c[R, 0:1], op.is_gt)
-    wf("ms", T.val3[:], 0.0)
-    iota("gn", T.nat[:], [[1, 16], [16, 24]], -192)
-    g.wait_ge(S.v, nones)
-    sel("gb", T.rst[:], T.ones[:, 0:125], [[0, 25], [1, 5]], op.is_gt, 0, 0)
+    iota(T.lo_r[:], [[0, H + 1], [COLS, N]])
+    iota(T.key_r[:], [[1, H + 1], [H, N]])
+    rows = iota(T.q_r[:], [[0, 2], [1, 16]])
+    nat = iota(T.nat[:], [[1, 16], [16, 24]], -192)
+    ones = v("ms", T.ones[:], 1.0)
+    for b in (T.val1[:], T.g1[:, 32:96], T.ln1[:], T.dn1[:, 0:32], T.big1[:, 0:1], T.f2[:, 125:128]):
+        v("ms", b, 0.0)
+    zero = v("ms", T.t3[:], 0)
+    v("tr", T.lo_c[:], T.lo_r[:, 0:32], after=[rows])
+    key = v("tr", T.key_c[:], T.key_r[:, 0:32])
+    v("tr", T.q_c[:], T.q_r[:])
+    v("ms", T.win1[:], 0.0)
+    lm = v("ts", T.lm[R, :], T.key_r[R, 0:32], T.key_c[R, 0:1], op.is_gt, after=[key])
+    fill(T.rst, 128, 0, 130, 1.0, after=[ones])
+    full = fill(T.rst8, 32, 0, 192, 1.0)
+    z2 = fill(T.z2, 128, 0, 32, 0.0)
+    c80 = fill(T.c80, 32, 0, 5, float(SLOT))
+    rst = fill(T.rst, 128, 0, 130, 0.0, step=N, after=[full])
+    fill(T.rst8, 32, 0, 192, 0.0, step=G)
+    for buf, tall, c0, c1, value in ((T.bmp, 128, 0, 32, 192.0), (T.cs2, 128, 0, 5, 128.0), (T.tb2, 128, 0, 128, 128.0),
+                                     (T.la3, 32, 0, 32, 0.0), (T.eb3, 32, 0, 32, 0.0),
+                                     (T.val3, 128, 0, 128, 0.0), (T.val3, 128, 128, 256, 0.0), (T.v3, 32, 0, W, 0.0),
+                                     (T.win3, 128, mine, mine + 192, 0.0), (T.win3, 128, mine + 192, mine + COLS, 0.0)):
+        filled = fill(buf, tall, c0, c1, value)
 
-    V.wait_ge(S.d_e1, 80)
-    v("ts", T.ab0[R, 32:96], T.e1[R, :], T.lo_c[R, 0:1], op.is_ge)
-    nab = vf("ts", T.ab1[R, 32:96], T.e1[R, :], -float(COLS), op.add, T.lo_c[R, 0:1], op.is_ge)
-    V.wait_ge(S.d_l, 16)
-    nlf = wf("cp", T.lf[:], T.l0[:])
-    g.sync.wait_ge(S.w, nlf)
-    g.sync.dma_start(T.lists[me], T.lf[:]).then_inc(S.d_lf, 16)
-    g.sync.wait_ge(S.v, nab)
-    g.sync.wait_ge(S.gn, cnt["gn"])
+    lists = send([(r, own, own) for r in order[:-1]], "sl", [l_own])
+    for a, b, base in ((0, rest, me + 1), (rest, N, 0)):
+        if b > a:
+            f2 = iota(T.f2[0:1, 25 * a:25 * b], [[1, b - a], [0, 5], [N, N]], base, after=[zero])
+    sa0 = sel(T.sa0[:], T.ones[0:32, 0:30], [[-H, 5], [0, H]], op.is_ge, 0, 1)
+    tb0 = iota(T.tb0[:], [[0, 5], [16, 5]], 128)
     for blk in range(2):
         for odd in range(2):
-            g.sync.dma_start(T.val1[16 * odd:128:32, 96 * blk:96 * blk + 96],
-                             T.nat[16 * odd:128:32, :, 32 * blk + 16 * odd:32 * blk + 16 * odd + 16]).then_inc(S.d_v1, 16)
+            l_v1 = dma("y", T.val1[16 * odd:128:32, 96 * blk:96 * blk + 96],
+                       T.nat[16 * odd:128:32, :, 32 * blk + 16 * odd:32 * blk + 16 * odd + 16], "d_v1", after=[zero, nat])
+    l_w = dma("y", T.wt[:], T.w[:], "d_w")
 
-    per = len(topo.engines(core, T.cores[others[0]])) // len(others)
-    landed = per * len(others)
+    v("ts", T.ab0[R, :], T.e1[R, :], T.lo_c[R, 0:1], op.is_ge, after=[l_e1, lm])
+    t = v("ts", T.ab1[R, :], T.e1[R, :], -float(COLS), op.add, T.lo_c[R, 0:1], op.is_ge)
+    big = v("ts", T.big1[R, 1:65], T.e1[R, :], T.lo_c[R, 0:1], op.is_ge, BIG, op.mult)
+    t = v("scan", T.c1[R, :], T.ab0[R, :], T.ab1[R, :], 0.0, op.add, op.subtract, after=[t])
+    v("ts", T.up1[R, 32:96], T.e1[R, :], T.lo_c[R, 0:1], op.is_ge, BIG + 1, op.mult)
+    t = v("ts", T.ln1[R, :], T.lm[R, :], T.c1[R, W - 1:W], op.mult, after=[t])
+    v("tt", T.dn1[R, 32:96], T.ab1[R, :], T.big1[R, 0:64], op.add, after=[big])
+    t = v("tr", T.up1[:, 0:32], T.ln1[:], after=[t])
+    g1 = v("scan", T.g1[R, :], T.up1[R, :], T.dn1[R, :], 0.0, op.add, op.subtract, after=[t])
+    for a in range(4):
+        bmp = act(T.bmp[32 * a:32 * a + N, :], T.ones[0:N, 0:32], LINE, scale=T.g1[0:N, 31:32], bias=-192.0, after=[filled, g1])
+    for b in range(G):
+        l_z = dma("y", T.z2[32 * (b // 2):32 * (b // 2) + 8, 16 * (b % 2):16 * (b % 2) + 16], T.f2[0:1, :], "d_z", after=[f2, z2])
 
-    def spread(src, dst, sem):
-        moves = []
-        for i, r in enumerate(others):
-            rid, pid, _ = topo.addr(T.cores[r])
-            e = topo.engines(core, T.cores[r])[per * i:per * i + per]
-            moves.append(RemoteDMATransfer(dst_ids=[DstId(rid=rid, pnc=pid)], dma_engine_mask=sum(1 << b for b in e),
-                                           remote_sem=sem, srcs=[src(r)], dsts=[dst]))
-        g.remote_dma_fused(moves, local_sem=S.loc)
-
-    iota("ge", T.thr_r[:], [[-2 * COLS, H + 1], [0, N]], 1)
-    iota("ge", T.run_r[:], [[0, H + 1], [-10 * SLOT, N]])
-    iota("ge", T.q_r[:], [[0, 2], [1, 16]])
-    iota("ge", T.tc0[:], [[16, 5]])
-    g.wait_ge(S.d_lf, 16)
-    spread(lambda r: T.lists[me], T.lists[me], S.sl)
-
-    sel("gd", T.sa0[:], T.ones[0:32, 0:30], [[-H, 5], [0, H]], op.is_ge, 0, 1)
-    sel("gd", T.mr0[:], T.ones[0:32, 0:5], [[-H, 5]], op.is_ge, 0, 1)
-    sel("gd", T.rst2[:], T.ones[:, 0:50], [[0, 5], [1, 10]], op.not_equal, -1, 0)
-    g.wait_ge(S.gd, cnt["gd"])
-    sel("gd", T.sam[:], T.sa0[:], [[H, 5], [0, H]], op.is_ge, H - 1, -1)
-    sel("gd", T.mr[:], T.mr0[:], [[H, 5]], op.is_ge, H - 1, -1)
-    g.wait_ge(S.gd, cnt["gd"])
-    sel("gd", T.lsa[:], T.sam[:], [[1, 30]], op.is_gt, 0, -1)
-    sel("gd", T.lst[:], T.sam[:], [[-1, 30]], op.is_gt, 0, 1)
-    sel("gd", T.rst6[:], T.ones[0:32, :], [[0, 24], [1, H]], op.is_gt, 0, 0)
-
-    v("scan", T.c1[R, :], T.ab0[R, 32:96], T.ab1[R, 32:96], 0.0, op.add, op.subtract)
-    wf("ms", T.win1[:, 0:200], 0.0)
-    v("ts", T.ln1[R, :], T.lm[R, :], T.c1[R, W - 1:W], op.mult)
-    wf("ms", T.win1[:, 200:400], 0.0)
-    v("tr", T.ab0[:, 0:32], T.ln1[:])
-    for b in ("t3", "bm2", "la3"):
-        wf("ms", T[b][:], 0.0)
-    nz = cnt["w"]
-    v("scan", T.g1[R, :], T.ab0[R, :], T.ab1[R, :], 0.0, op.add, op.subtract)
-
-    def pack(b):
-        return wf("qz", T.q[:, 128 * b:128 * b + 128], T.p[:, 128 * b:128 * b + 128], T.xt[:, 512 * b:512 * b + 512])
-    V.wait_ge(S.d_x, 32)
-    pack(0)
-    v("tt", T.z1[R, :], T.g1[R, 32:96], T.ab0[R, 32:96], op.mult)
+    def pack(b, after=()):
+        return v("qz", T.q[:, 128 * b:128 * b + 128], T.p[:, 128 * b:128 * b + 128], T.xt[:, 512 * b:512 * b + 512], after=after)
+    t = v("tr", T.zt1[:], T.g1[:, 32:96], after=[g1])
+    pack(0, [l_x])
+    v("scan", T.s1[:, 0:30], T.rst[0:32, 0:30], T.zt1[:, 0:30], 0.0, op.mult, op.max, after=[t, rst])
+    t = v("scan", T.s1[:, 30:60], T.rst[0:32, 0:30], T.zt1[:, 32:62], 0.0, op.mult, op.max)
     pack(1)
-    v("tr", T.zt1[:], T.z1[:])
-    n1 = pack(2)
-    V.wait_ge(S.gb, cnt["gb"])
-    v("scan", T.s1[:, 0:30], T.rst[0:32, 0:30], T.zt1[:, 0:30], 0.0, op.mult, op.max)
-    vf("scan", T.s1[:, 30:60], T.rst[0:32, 0:30], T.zt1[:, 32:62], 0.0, op.mult, op.max)
-    wf("ms", T.cs2[:], -128.0)
-    v("ts", T.of1[0:32, :], T.s1[:, 4:60:5], -1.0, op.add)
-    for a in range(1, 4):
-        vf("ts", T.of1[32 * a:32 * a + 32, :], T.s1[:, 4:60:5], -1.0, op.add)
-    V.wait_ge(S.w, n1)
-    V.wait_ge(S.d_v1, 64)
-    nw1 = v("cp", T.win1[:, 0:400].indirect(T.of1[:, 0:12]), T.val1[:])
-    A.wait_ge(S.v, nw1)
-    V.wait_ge(S.ge, cnt["ge"])
-    nct = wf("tr", T.thr_c[:], T.thr_r[:, 0:32])
-    V.wait_ge(S.v, nw1)
-    for k in range(N):
+    for a in range(4):
+        of1 = v("ts", T.of1[32 * a:32 * a + 32, :], T.s1[:, 4:60:5], -1.0 - BIG, op.add, after=[t])
+    rowp = v("tr", T.rowp[:], T.bmp[:], after=[bmp])
+    win1 = v("cp", T.win1[:, 0:400].indirect(T.of1[:, 0:12]), T.val1[:], after=[of1, l_v1])
+    packed = pack(2)
+
+    counts = send([(r, T.rowp[:, 0:8], T.land[:, me, :]) for r in order[:-1]], "sp", [rowp])
+    sam = sel(T.sam[:], T.sa0[:], [[H, 5], [0, H]], op.is_ge, H - 1, -1, after=[sa0])
+    mx0 = sel(T.mx0[:], T.c80[:], [[-H, 5]], op.is_ge, 0, 1, after=[c80])
+    low = sel(T.low[:], T.ones[0:32, 0:5], [[-H, 5]], op.is_ge, -H, 1)
+    sel(T.lsa[:], T.sam[:], [[1, 30]], op.is_gt, 0, -1, after=[sam])
+    sel(T.mx[:], T.mx0[:], [[H, 5]], op.is_ge, H - 1, -1, after=[mx0])
+    tables = iota(T.t80[:], [[SLOT, N], [0, N]])
+    act(T.land[:, me, :], T.rowp[:, 0:8], COPY, after=[rowp])
+
+    l_e3 = dma("y", T.e3[R, :], T.lists[:], "d_e3", after=[lists, l_own])
+    for b, a0, a1, row in [(b, 4 * b, min(4 * b + 4, N * H), 0) for b in range(G)] + [(G - 1, 0, 2, 8)]:
+        top = 32 * (b // 2) + row
+        l_t3 = dma("y", T.t3[top:top + 4 * (a1 - a0), 16 * (b % 2):16 * (b % 2) + 16], T.e3[a0:a1, :], "d_t3", after=[l_e3, zero])
+
+    for i, k in enumerate(order):
         for u in (0, 16):
-            out, in_ = T.dup1[:, 5 * k:5 * k + 5, u:u + 16], T.win1[:, k:400:5]
-            if k < 3:
-                vf("cp", out, in_)
+            out, in_ = T.dup1[:, 5 * i:5 * i + 5, u:u + 16], T.win1[:, k:400:5]
+            if i < 3:
+                t = v("cp", out, in_, after=[win1])
             else:
-                nd1 = act(out, in_, COPY)
-    V.wait_ge(S.ac, nd1)
-    v("tr", T.tr1[:], T.dup1[:])
-    wf("tr", T.q_c[:], T.q_r[:])
-    nrc = wf("tr", T.run_c[:], T.run_r[:, 0:32])
-    v("tt", T.sm1[:], T.tr1[:, 0:800:32], T.tr1[:, 16:800:32], op.add)
-    w("ts", T.tcw[:], T.tc0[:], T.q_c[:, 0:1], op.add)
-    nl1 = v("ts", T.l1[:, 0:25], T.sm1[:], 192.0, op.add)
-    w("ts", T.tcb[:], T.tcw[:], 0.5, op.add, STEP, op.mult)
-    k1 = v("cp", T.q2[:].bitcast(dt.uint32), T.q[:].bitcast(dt.uint32).indirect(T.l1[:, 0:25]))
-    A.wait_ge(S.w, n1)
-    A.wait_ge(S.v, nl1)
-    A.activation(T.p2[:], T.p[:].indirect(T.l1[:, 0:25]), COPY).then_inc(S.ap, 1)
+                dup = act(out, in_, COPY, after=[win1])
+    t = v("tr", T.tr1[:], T.dup1[:], after=[t, dup])
+    t = v("tt", T.sm1[:], T.tr1[:, 0:800:32], T.tr1[:, 16:800:32], op.add, after=[t])
+    l1 = v("ts", T.l1[:, 0:25], T.sm1[:], 192.0, op.add, after=[t])
 
-    cut = lambda r, n: slice(SLOT * r, SLOT * r + n)
-    g.wait_ge(S.v, k1)
-    spread(lambda r: T.q2[:, cut(r, SENT1)].bitcast(dt.uint8), T.ql[:, cut(me, SENT1)].bitcast(dt.uint8), S.s1c)
-    g.wait_ge(S.ap, 1)
-    spread(lambda r: T.p2[:, cut(r, SENT1)], T.pl[:, cut(me, SENT1)], S.s1p)
+    def hop(cw, pw, lst, co, po, cl, pl, n, sc, sp, for_codes, for_planes, between=None):
+        u8 = lambda a: a.bitcast(dt.uint8)
+        for i in range(2):
+            kc = codes(co[:, 160 * i:160 * i + 160], cw, lst[:, 10 * i:10 * i + 10], for_codes)
+            kp = planes(po[:, 160 * i:160 * i + 160], pw, lst[:, 10 * i:10 * i + 10], for_planes)
+            if between and i == 0:
+                between()
+            come = send([(order[j], u8(co[:, cut(j, n)]), u8(cl[:, cut(me, n)])) for j in (2 * i, 2 * i + 1)], sc, [kc])
+        return come, send([(r, po[:, cut(j, n)], pl[:, cut(me, n)]) for j, r in enumerate(order[:-1])], sp, [kp])
 
-    g.sync.wait_ge(S.w, nz)
-    g.sync.wait_ge(S.sl, landed)
-    g.sync.wait_ge(S.d_lf, 16)
-    for d in range(N + 1):
-        g.sync.dma_start(T.e2[N * d:N * d + N, :], T.lists[:]).then_inc(S.d_e2, 16)
-    g.sync.dma_start(T.e3[R, :], T.lists[:]).then_inc(S.d_e3, 16)
-    g.sync.wait_ge(S.d_e3, 16)
-    for b in range(8):
-        g.sync.dma_start(T.t3[32 * (b // 2):32 * (b // 2) + 20, 16 * (b % 2):16 * (b % 2) + 16],
-                         T.e3[5 * (b % H):5 * (b % H) + 5, :]).then_inc(S.d_t3, 16)
-    g.sync.wait_ge(S.v, k1)
-    g.sync.dma_start(T.ql[:, cut(me, SLOT)].bitcast(dt.uint8), T.q2[:, cut(me, SLOT)].bitcast(dt.uint8)).then_inc(S.d_o1, 16)
-    g.sync.wait_ge(S.ap, 1)
-    g.sync.dma_start(T.pl[:, cut(me, SLOT)], T.p2[:, cut(me, SLOT)]).then_inc(S.d_o1, 16)
+    c1, p1 = hop(T.q, T.p, T.l1, T.q2, T.p2, T.ql, T.pl, SENT1, "s1c", "s1p", [l1], [l1, packed])
 
-    A.wait_ge(S.d_e2, 96)
-    A.wait_ge(S.w, nct)
-    nsg = act(T.jk2[R, :], T.e2[R, :], FN.Sign, scale=2.0, bias=T.thr_c[R, 0:1], accum_out=T.sg2[R, 0:1])
-    A.wait_ge(S.d_e3, 16)
-    nu3 = act(T.u3[R, :], T.e3[R, :], FN.Abs, scale=2.0, bias=-float(2 * COLS * me + COLS - 1))
-    A.wait_ge(S.ac, nsg)
-    A.wait_ge(S.w, nrc)
-    for a in range(2):
-        nbm = act(T.bm2[32 * a:32 * a + 30, :], T.ones[R, 0:32], LINE, scale=T.sg2[R, 0:1], bias=T.run_c[R, 0:1])
-    A.wait_ge(S.ac, nu3)
-    ni3 = act(T.aa3[R, 32:96], T.u3[R, :], FN.Sign, scale=-1.0, bias=float(COLS), accum_out=T.na3[R, 0:1])
-    A.wait_ge(S.gd, cnt["gd"])
-    A.wait_ge(S.ac, ni3)
-    nla = act(T.la3[R, 0:30], T.lsa[R, :], LINE, scale=T.na3[R, 0:1])
+    v("ts", T.ea3[R, 32:96], T.e3[R, :], float(mine), op.is_ge, after=[l_e3])
+    a3 = v("ts", T.eb3[R, 32:96], T.e3[R, :], float(mine + COLS), op.is_ge)
+    zc = v("tr", T.zc2[:], T.z2[:], after=[l_z])
+    nn = v("tt", T.nn2[:], T.land[:, :, 1:6], T.land[:, :, 0:5], op.subtract, after=[counts])
+    xa = v("tt", T.xo3[R, 0:5], T.land[R, :, me], T.mx[R, :], op.mult, after=[tables])
+    tb2 = act(T.tb2[:, 0:125:5], T.tb0[:], LINE, bias=T.q_c[:, 0:1], after=[tb0])
+    act(T.jk3[R, 15:20], T.low[R, :], LINE, scale=-128.0, bias=3016.0, accum_out=T.gb3[R, 0:1], after=[tables])
+    own_p1 = planes(T.pl[:, cut(me, SLOT)], T.p, T.l1[:, 20:25])
+    cp = act(T.jk3[R, 0:5], T.xo3[R, 0:5], LINE, scale=0.0025, bias=7.56, accum_out=T.cp3[R, 0:1], after=[xa])
+    a3 = v("scan", T.c3[R, :], T.ea3[R, 32:96], T.eb3[R, 32:96], 0.0, op.add, op.subtract, after=[a3])
+    of2 = v("cp", T.of2[:], T.zc2[:, 0:8], after=[zc])
+    cs = v("ts", T.cs2[:, 5:30], T.nn2[:], 0.2, op.mult, 128.4, op.add, after=[nn])
+    ci = v("ts", T.ci0[:], T.land[:, :, 0:5], 0.2, op.mult, 38.8 - 0.2 * me, op.add)
+    a3 = v("ts", T.la3[R, 0:30], T.lsa[R, :], T.c3[R, W - 1:W], op.mult, after=[a3])
+    xb = v("tt", T.xo3[R, 5:10], T.cs2[R, 5 + me:30:5], T.low[R, :], op.mult, after=[cs])
+    b2 = v("tt", T.d2[:], T.cs2[:, 0:30].indirect(T.of2[:]), T.tb2[:], op.subtract, after=[of2, tb2])
+    cv = act(T.jk3[R, 5:15], T.xo3[R, :], LINE, accum_out=T.cv3[R, 0:1], after=[xb])
+    a3 = v("tr", T.ea3[:, 0:32], T.la3[:], after=[a3])
+    ci = v("tt", T.ci2[:, 0:25], T.ci0[:], T.t80[:], op.add, after=[ci])
+    u2 = v("scan", T.u2[:], T.rst[:, 0:128], T.d2[:], 0.0, op.mult, op.add, after=[b2])
+    gx = act(T.gx2[:], T.u2[:], LINE, scale=-STEP, bias=STEP / 2, after=[u2])
+    g3 = v("scan", T.g3[R, :], T.ea3[R, :], T.eb3[R, :], 0.0, op.add, op.subtract, after=[a3])
+    gv = act(T.gv3[R, :], T.g3[R, 32:96], LINE, scale=float(SLOT), bias=T.gb3[R, 0:1], after=[g3, cp])
+    b2 = v("tt", T.fx2[:], T.ci2[:, 0:25].indirect(T.of2[:]), T.u2[:], op.subtract, after=[u2, ci])
+    v("ts", T.pp3[R, :], T.g3[R, 32:96], 0.2, op.mult, T.cp3[R, 0:1], op.add, after=[g3, cp])
+    a3 = v("ts", T.qq3[R, :], T.g3[R, 32:96], 0.2, op.mult, -0.6, op.add)
+    b2 = v("scan", T.ss2[:], T.gx2[:, 0:125], T.fx2[:, 0:125], 0.0, op.max, op.min, after=[b2, gx])
+    v("ts", T.tp3[R, :], T.pp3[R, :], -400.0, op.mult, T.cv3[R, 0:1], op.add, after=[a3, cv])
+    a3 = v("tt", T.ts3[R, :], T.gv3[R, :], T.qq3[R, :], op.add, after=[gv])
+    l2 = v("ts", T.l2[:, 0:25], T.ss2[:, 4:125:5], float(SLOT * (N - 1) + SENT1 - 1), op.min, after=[b2])
+    own_c1 = codes(T.ql[:, cut(me, SLOT)], T.q, T.l1[:, 20:25])
+    v3 = v("tt", T.v3[R, :], T.tp3[R, :], T.ts3[R, :], op.add, after=[a3])
+    l_v3 = dma("y", T.val3[0:128:16, :], T.v3[:], "d_v3", after=[v3, filled])
+    at = {"t": v("cp", T.tf3[:], T.t3[:], after=[l_t3])}
 
-    wf("ms", T.cs2[:, 1:50:10], 0.0)
-    V.wait_ge(S.gd, cnt["gd"])
-    wf("ts", T.bb3[R, 0:30], T.lst[R, :], float(W), op.mult)
-    wf("ms", T.bb3[:, 30:32], 0.0)
-    wf("ms", T.bb3[:, 32:96], 1.0)
-    wf("ts", T.mx[R, :], T.mr[R, :], -40.0, op.mult)
-    V.wait_ge(S.ac, nsg)
-    for a in range(2, 4):
-        vf("ts", T.bm2[32 * a:32 * a + 30, :], T.ones[R, 0:32], T.sg2[R, 0:1], op.mult, T.run_c[R, 0:1], op.add)
-    V.wait_ge(S.ac, nbm)
-    v("tr", T.row2[:], T.bm2[:])
-    v("tt", T.nn2[:], T.row2[:, 0:25], T.row2[:, 5:30], op.subtract)
-    vf("ts", T.ci2[:], T.row2[:, 0:25], -0.1, op.mult, 38.8 - 0.2 * me, op.add)
-    v("ts", T.cs2[:, 2:50:2], T.nn2[:, 0:24], 0.1, op.mult, 128.4, op.add)
-    V.wait_ge(S.ac, nla)
-    wf("tr", T.aa3[:, 0:32], T.la3[:])
-    V.wait_ge(S.w, cnt["w"] - 1)
-    v("scan", T.o2[:], T.rst2[:], T.cs2[:], 0.0, op.mult, op.add)
-    ng3 = w("scan", T.g3[R, :], T.aa3[R, :], T.bb3[R, :], 0.0, op.add, op.add)
-    noff = v("tt", T.off2[:], T.ci2[:], T.o2[:, 1:50:2], op.subtract)
-    vf("tt", T.xo3[R, 0:5], T.row2[R, 5 * me:5 * me + 5], T.mx[R, :], op.mult)
-    nxo = vf("tt", T.xo3[R, 5:10], T.o2[R, 10 * me + 1:10 * me + 10:2], T.mr[R, :], op.mult)
-    nqq = w("ts", T.qq3[R, :], T.g3[R, 32:96], 0.1, op.mult, -0.6, op.add)
-    A.wait_ge(S.w, ng3)
-    ngv = act(T.gv3[R, :], T.g3[R, 32:96], LINE, scale=40.0, bias=15080.0)
-    A.wait_ge(S.v, nxo)
-    ncp = act(T.jk3[R, 0:5], T.xo3[R, 0:5], LINE, scale=0.0025, bias=7.56, accum_out=T.cp3[R, 0:1])
-    ncv = act(T.jk3[R, 5:15], T.xo3[R, :], LINE, accum_out=T.cv3[R, 0:1])
-    for j in range(N):
-        nfx = act(T.fx2[:, 25 * j:25 * j + 25], T.off2[:], LINE, bias=T.tcw[:, j:j + 1])
-    for j in range(N):
-        vf("ts", T.gx2[:, 25 * j:25 * j + 25], T.o2[:, 1:50:2], -STEP, op.mult, T.tcb[:, j:j + 1], op.add)
-    V.wait_ge(S.ac, ncp)
-    npp = wf("ts", T.pp3[R, :], T.g3[R, 32:96], 0.1, op.mult, T.cp3[R, 0:1], op.add)
-    V.wait_ge(S.w, nqq)
-    wf("tt", T.ts3[R, :], T.gv3[R, :], T.qq3[R, :], op.add)
-    V.wait_ge(S.w, npp)
-    V.wait_ge(S.ac, ncv)
-    wf("ts", T.tp3[R, :], T.pp3[R, :], -400.0, op.mult, T.cv3[R, 0:1], op.add)
-    V.wait_ge(S.ac, nfx)
-    v("scan", T.ss2[:], T.gx2[:], T.fx2[:], 0.0, op.max, op.min)
-    nv3 = w("tt", T.v3[R, :], T.tp3[R, :], T.ts3[R, :], op.add)
-    V.wait_ge(S.v, cnt["v"])
-    for j in range(N):
-        n2 = vf("ts", T.l2[:, j:25:5], T.ss2[:, 25 * j + 4:25 * j + 25:5], float(SLOT * (N - 1) + SENT1 - 1), op.min)
+    def between():
+        at["t"] = v("tr", T.tr0[:], T.tf3[:], after=[at["t"]])
+    c2, p2 = hop(T.ql, T.pl, T.l2, T.q3, T.p3, T.qm, T.pm, SLOT, "s2c", "s2p", [l2, own_c1, c1], [l2, own_p1, p1], between)
+    own_p2 = planes(T.pm[:, cut(me, SLOT)], T.pl, T.l2[:, 20:25])
 
-    V.wait_ge(S.v, n2)
-    V.wait_ge(S.s1c, landed)
-    V.wait_ge(S.d_o1, 32)
-    k2 = v("cp", T.q3[:].bitcast(dt.uint32), T.ql[:].bitcast(dt.uint32).indirect(T.l2[:, 0:25]))
-    A.wait_ge(S.v, n2)
-    A.wait_ge(S.s1p, landed)
-    A.wait_ge(S.d_o1, 32)
-    A.activation(T.p3[:], T.pl[:].indirect(T.l2[:, 0:25]), COPY).then_inc(S.ap, 1)
-    g.wait_ge(S.v, k2)
-    spread(lambda r: T.q3[:, cut(r, SLOT)].bitcast(dt.uint8), T.qm[:, cut(me, SLOT)].bitcast(dt.uint8), S.s2c)
-    g.wait_ge(S.ap, 2)
-    spread(lambda r: T.p3[:, cut(r, SLOT)], T.pm[:, cut(me, SLOT)], S.s2p)
-    g.sync.wait_ge(S.w, nv3)
-    g.sync.dma_start(T.val3[0:96:16, :], T.v3[R, :]).then_inc(S.d_v3, 16)
-    g.sync.wait_ge(S.v, k2)
-    g.sync.dma_start(T.qm[:, cut(me, SLOT)].bitcast(dt.uint8), T.q3[:, cut(me, SLOT)].bitcast(dt.uint8)).then_inc(S.d_o2, 16)
-    g.sync.wait_ge(S.ap, 2)
-    g.sync.dma_start(T.pm[:, cut(me, SLOT)], T.p3[:, cut(me, SLOT)]).then_inc(S.d_o2, 16)
-
-    V.wait_ge(S.d_t3, 128)
-    nt0 = wf("tr", T.tr0[:], T.t3[:])
-    V.wait_ge(S.d_w, 16)
-    wf("qz", T.wq[:], T.wp[:], T.wt[:])
-    mine = COLS * me
-    wf("ms", T.win3[:, mine:mine + COLS], 0.0)
-    V.wait_ge(S.w, nt0)
-    wf("cp", T.of3[:], T.tr0[:, 0:20])
-    V.wait_ge(S.d_v3, 16)
-    nw3 = w("cp", T.win3[:].indirect(T.of3[:]), T.val3[:])
-    A.wait_ge(S.w, nw3)
-    nd3 = act(T.dup3[:, 12:24, 16:32], T.win3[:, mine + 192:mine + 384], COPY)
-    w("cp", T.dup3[:, :, 0:16], T.win3[:, mine:mine + 384])
-    wf("cp", T.dup3[:, 0:12, 16:32], T.win3[:, mine:mine + 192])
-    V.wait_ge(S.ac, nd3)
-    nt3 = w("tr", T.tr3[:], T.dup3[:])
-    A.wait_ge(S.w, nt3)
-    V.wait_ge(S.w, nt3)
-    for r in range(H):
-        out, in_ = T.su3[:, r:144:6], T.tr3[32 * (r // 2):32 * (r // 2) + 32, 16 * (r % 2):768:32]
-        if r < 3:
-            wf("cp", out, in_)
+    of3 = v("cp", T.of3[:], T.tr0[:, 0:16], after=[at["t"]])
+    codes(T.qm[:, cut(me, SLOT)], T.ql, T.l2[:, 20:25])
+    win3 = v("cp", T.win3[:].indirect(T.of3[:]), T.val3[:], after=[of3, l_v3])
+    v("qz", T.wq[:, 0:128], T.wp[:, 0:128], T.wt[:, 0:512], after=[l_w])
+    dup = act(T.dup3[:, 12:24, 16:32], T.win3[:, mine + 192:mine + 384], COPY, after=[win3])
+    v("cp", T.dup3[:, :, 0:16], T.win3[:, mine:mine + 384], after=[win3])
+    t = v("cp", T.dup3[:, 0:12, 16:32], T.win3[:, mine:mine + 192])
+    wq = v("qz", T.wq[:, 128:256], T.wp[:, 128:256], T.wt[:, 512:1024])
+    tr3 = v("tr", T.tr3[:], T.dup3[:], after=[t, dup])
+    for r in range(G):
+        out, in_ = T.su3[:, r:192:G], T.tr3[32 * (r // 2):32 * (r // 2) + 32, 16 * (r % 2):768:32]
+        if r < G // 2:
+            t = v("cp", out, in_, after=[tr3])
         else:
-            nsu = act(out, in_, COPY)
-    V.wait_ge(S.ac, nsu)
-    w("scan", T.sv3[:], T.rst6[:], T.su3[:], 0.0, op.mult, op.add)
-    w("ts", T.l3[0:32, :], T.sv3[:, 5:144:6], 200.0, op.add)
-    for a in range(1, 4):
-        n3 = wf("ts", T.l3[32 * a:32 * a + 32, :], T.sv3[:, 5:144:6], 200.0, op.add)
+            su = act(out, in_, COPY, after=[tr3])
+    t = v("scan", T.sv3[:], T.rst8[:], T.su3[:], 0.0, op.mult, op.add, after=[t, su])
+    for a in range(4):
+        l3 = v("ts", T.l3[32 * a:32 * a + 32, :], T.sv3[:, G - 1:192:G], 200.0, op.add, after=[t])
 
-    V.wait_ge(S.s2c, landed)
-    V.wait_ge(S.d_o2, 32)
-    V.wait_ge(S.w, n3)
-    A.wait_ge(S.w, n3)
-    A.wait_ge(S.s2p, landed)
-    A.wait_ge(S.d_o2, 32)
+    wait("m", [wq, own_p2, c2, p2])
+    res, copied, part = (T.rs0, T.rs1), [], N * SLOT // 2
+    for b in range(4):
+        o, c, bank = b // 2, slice(part * (b % 2), part * (b % 2) + part), T.ps[:, 512 * b:512 * b + part]
+        t = mark(g.tensor.matmul_mx(bank, T.wq[:, 128 * o:128 * o + 128], T.wp[:, 128 * o:128 * o + 128],
+                                    T.qm[:, c], T.pm[:, c], True, True), "m", 1)
+        copied.append(act(res[o][:, c], bank, COPY, after=[t]) if b % 2 else v("cp", res[o][:, c], bank, after=[t]))
     HALF = COLS // 2
     for h in range(2):
-        c = slice(HALF * h, HALF * h + HALF)
-        off = T.l3[:, 12 * h:12 * h + 12]
-        nk = vf("cp", T.q4[:, c].bitcast(dt.uint32), T.qm[:].bitcast(dt.uint32).indirect(off))
-        A.activation(T.p4[:, c], T.pm[:].indirect(off), COPY).then_inc(S.ap, 1)
-        g.tensor.wait_ge(S.v, nk)
-        g.tensor.wait_ge(S.ap, 3 + h)
         for o in range(2):
-            b = 2 * h + o
-            g.tensor.matmul_mx(T.ps[:, 512 * b:512 * b + HALF], T.wq[:, 128 * o:128 * o + 128], T.wp[:, 128 * o:128 * o + 128],
-                               T.q4[:, c], T.p4[:, c], True, True).then_inc(S["m%d" % b], 1)
-    for h in range(2):
-        for o in range(2):
-            b = 2 * h + o
-            y = T.ys[:, COLS * o + HALF * h:COLS * o + HALF * h + HALF]
-            out = T.y[:, COLS * o + HALF * h:COLS * o + HALF * h + HALF]
-            if o == 0:
-                V.wait_ge(S["m%d" % b], 1)
-                ny = vf("cp", y, T.ps[:, 512 * b:512 * b + HALF])
-                g.sync.wait_ge(S.v, ny)
-                g.sync.dma_start(out, y).then_inc(S.st, 16)
+            c = slice(COLS * o + HALF * h, COLS * o + HALF * h + HALF)
+            pick, need = res[o][:].indirect(T.l3[:, 12 * h:12 * h + 12]), copied[2 * o:2 * o + 2] + [l3]
+            t = act(T.ys[:, c], pick, COPY, after=need) if o else v("cp", T.ys[:, c], pick, after=need)
+            if o and h:
+                wait("a", [dma("a", T.y[:, c], T.ys[:, c], "st2", after=[t])])
             else:
-                A.wait_ge(S["m%d" % b], 1)
-                ny = act(y, T.ps[:, 512 * b:512 * b + HALF], COPY)
-                A.wait_ge(S.ac, ny)
-                A.dma_start(out, y).then_inc(S.st2, 16)
-    g.sync.wait_ge(S.st, 32)
-    A.wait_ge(S.st2, 32)
-    g.wait_ge(S.v, cnt["v"])
-    g.wait_ge(S.w, cnt["w"])
-    g.wait_ge(S.loc, 5 * landed)
+                stored = dma("y", T.y[:, c], T.ys[:, c], "st", after=[t])
+    wait("y", [stored])
+    wait("g", [(s, count[s]) for s in ("v", "g", "loc")])

@@ -4,34 +4,38 @@ from concourse.mybir import dt, AluOpType, ActivationFunctionType
 N, COLS = 5, 384
 SLOT = 80
 SENT1 = 78
-H = 6
-W = COLS // H
+U = 12
 STEP = 1024.0
-BIG = 512.0
-G = 8
-PER = 4 * W
+NB = N - 1
 
 F32, BF, I32, U16 = "float32", "bfloat16", "int32", "uint16"
 X4, U8 = "float8_e4m3fn_x4", "uint8"
 SMALL = {
     X4: "q:128,384 wq:128,256 q2:128,320 ql:128,400 q3:128,320 qm:128,400",
     U8: "p:128,384 wp:128,256 p2:128,320 pl:128,400 p3:128,320 pm:128,400",
-    BF: "xt:128,1536 wt:128,1024 nat:128,6,64 val1:128,192 win1:128,400 dup1:128,25,32 tr1:128,800 bmp:128,32 rowp:128,32 "
-        "land:128,5,8 cs2:128,32 v3:32,64 val3:128,256 win3:128,1920 dup3:128,24,32 tr3:128,768 rst8:32,192 su3:32,192 sv3:32,192",
-    I32: "e1:32,64 ci0:128,25 ci2:128,32 e3:32,64 t3:128,32 pp3:32,64 qq3:32,64",
-    U16: "of1:128,12 l1:128,26 of2:128,8 l2:128,26 of3:128,16 l3:128,24",
-    F32: "ys:128,768 rs0:128,400 rs1:128,400 lo_r:32,35 key_r:32,35 q_r:128,32 lo_c:32,32 key_c:32,32 q_c:128,32 ones:128,192 "
-         "rst:128,130 lm:32,32 ab0:32,64 ab1:32,64 big1:32,65 up1:32,96 dn1:32,96 c1:32,64 ln1:32,32 g1:32,96 zt1:32,64 s1:32,60 "
-         "sm1:128,25 f2:32,128 z2:128,32 zc2:128,32 tb0:128,25 tb2:128,128 t80:128,25 nn2:128,25 d2:128,128 u2:128,128 gx2:128,128 "
-         "fx2:128,128 ss2:128,125 sa0:32,30 sam:32,30 lsa:32,30 c80:32,5 mx0:32,5 mx:32,5 low:32,5 gb3:32,1 ea3:32,96 eb3:32,96 "
-         "c3:32,64 la3:32,32 g3:32,96 gv3:32,64 xo3:32,10 jk3:32,20 cp3:32,1 cv3:32,1 tp3:32,64 ts3:32,64 tf3:128,32 tr0:128,32",
+    BF: "xt:128,1536 wt:128,1024 val1:128,192 win1:128,400 dup1:128,25,32 tr1:128,800 bml:128,32 bmc:128,32 rowp:128,48 "
+        "land:128,80 ci0:128,70 ja:128,8 v3:128,32 val3:128,512 win3:128,1920 dup3:128,24,32 "
+        "tr3:128,768 su3:32,192 rst8:32,192 sw3:32,192",
+    I32: "e:128,32 pc:128,16 ti:128,16 jw:128,8 a3:128,32 b3:128,32",
+    U16: "tu:128,16 of1:128,12 l1:128,26 of2:128,8 l2:128,26 of3:128,16 l3:128,24",
+    F32: "ys:128,768 rs0:128,400 rs1:128,400 ones:128,128 ramp:128,16 fifth:128,32 thr:128,96 ge:128,112 cb:128,544 yy:128,97 "
+         "s4:128,65 bt:128,32 xs:128,96 cg:128,96 cand:128,96 sc:128,96 n1:128,1 sm1:128,25 qf:128,1 "
+         "col:128,16 jz:128,8 jt:128,8 rst:128,128 tb0:128,25 tb2:128,128 t80:128,72 ci2:128,70 d2:128,128 u2:128,128 "
+         "gx2:128,128 fx2:128,128 ss2:128,125 sel:128,10 xo:128,10 jk:128,16 ea:128,32 z:128,64 m3:128,32 "
+         "tp3:128,32",
 }
-SCRATCH = {"ps": ("psum", [128, 2048], F32), "lists": ("dram", [N * 128, 3], I32)}
+SCRATCH = {"ps": ("psum", [128, 2048], F32), "mine": ("dram", [128, 3], I32), "lists": ("dram", [NB * 128, 3], I32)}
 for _t in SMALL:
     for _b in SMALL[_t].split():
         SCRATCH[_b.split(":")[0]] = ("sbuf", [int(_n) for _n in _b.split(":")[1].split(",")], _t)
-SEMAPHORES = ["v", "a", "g", "m", "d_e1", "d_x", "d_w", "d_l", "d_z", "d_e3", "d_t3", "d_v1", "d_v3",
-              "sl", "sp", "s1c", "s1p", "s2c", "s2p", "loc", "st", "st2"]
+SEMAPHORES = ["v", "a", "g", "m", "d_e1", "d_x0", "d_x1", "d_x2", "d_w", "d_l", "d_e3", "d_o", "d_v3",
+              "sl", "sp", "s1c", "s1p", "s2a", "s2b", "s2p", "loc", "st", "st2"]
+
+FIRST = """ge tc c1 xs win0 p96 trl cg s4 tu8 counts1 jz base back cand x0 order rowl of1 rowc x1 win1 counts"""
+ORDER = """x2 turn2 turn3 turn0 turn1 turn4 jw trb of2 sumb tra l1b suma codes1b l1a ge3 trc planes1 d2 scan3 codes1a
+rest3 is below u2 tr3 xo ci2 sumc m3 fx2 a3 b3 l1c ss2 tp3 val0 v3 l2 own1 planes2 rows of3
+codes2a codes2b win3 own2 w0 wide w1 trw blocks sum8 l3"""
+PIECES = (("v", 0, 0, 8), ("a", 1, 0, 10), ("v", 0, 8, 24), ("a", 1, 10, 24))
 
 
 def cut(r, n):
@@ -49,9 +53,10 @@ def rank_program(g, core, T, topo):
     rest = N - 1 - me
     far = topo.engines(core, T.cores[order[0]])
     queues = {"v": V, "a": A, "g": g, "y": Y, "m": g.tensor}
-    count, seen = {}, {}
+    count, seen, k = {}, {}, {}
     CALL = {"ts": V.tensor_scalar, "tt": V.tensor_tensor, "cp": V.tensor_copy, "ms": V.memset,
             "scan": V.tensor_tensor_scan, "tr": V.transpose, "qz": V.quantize_mx}
+    BLK = [slice(32 * a, 32 * a + 32) for a in range(NB)]
 
     def wait(q, marks):
         for sem, n in marks:
@@ -71,20 +76,15 @@ def rank_program(g, core, T, topo):
             args = (out, a, s1, None, o1) if len(args) == 4 else (out, a, s1, args[4], o1, args[5])
         return mark(CALL[name](*args), "v", 1)
 
-    def act(out, in_, func, after=(), **k):
+    def act(out, in_, func=LINE, after=(), **kw):
         wait("a", after)
-        return mark(A.activation(out, in_, func, **k), "a", 1)
+        return mark(A.activation(out, in_, func, **kw), "a", 1)
 
-    def fill(buf, rows, c0, c1, value, step=1, after=()):
-        return act(buf[0:rows, c0:c1:step], T.ones[0:rows, 0:(c1 - c0) // step], COPY, scale=value, after=after)
+    def fill(out, n, value, after=()):
+        return act(out, T.ones[:, 0:n], COPY, scale=value, after=after)
 
-    def iota(out, pattern, base=0, after=()):
-        wait("g", after)
-        return mark(g.iota(out, pattern, base, 0, allow_small_or_imprecise_dtypes=True), "g", 1)
-
-    def sel(out, in_, pattern, how, base, cm, after=()):
-        wait("g", after)
-        return mark(g.affine_select(out, in_, pattern, how, 0.0, base, cm), "g", 1)
+    def iota(out, pattern, base, cm):
+        return mark(g.iota(out, pattern, base, cm, allow_small_or_imprecise_dtypes=True), "g", 1)
 
     def dma(q, out, in_, sem, after=()):
         wait(q, after)
@@ -107,191 +107,237 @@ def rank_program(g, core, T, topo):
         for s in (sem, "loc"):
             count[s] = count.get(s, 0) + len(far)
         return sem, count[sem]
-    R = slice(0, N * H)
-    own, mine = T.lists[128 * me:128 * me + 128, :], COLS * me
 
-    l_own = dma("y", own, T.to[:], "d_l")
-    for d in range(N):
-        l_e1 = dma("y" if d % 2 else "a", T.e1[d:N * H:N, :], T.to[:], "d_e1")
-    dma("y", T.xt[:, 0:768], T.x[:, 0:768], "d_x")
-    l_x = dma("a", T.xt[:, 768:1536], T.x[:, 768:1536], "d_x")
+    def u8(a):
+        return a.bitcast(dt.uint8)
 
-    iota(T.lo_r[:], [[0, H + 1], [COLS, N]])
-    iota(T.key_r[:], [[1, H + 1], [H, N]])
-    rows = iota(T.q_r[:], [[0, 2], [1, 16]])
-    nat = iota(T.nat[:], [[1, 16], [16, 24]], -192)
-    ones = v("ms", T.ones[:], 1.0)
-    for b in (T.val1[:], T.g1[:, 32:96], T.ln1[:], T.dn1[:, 0:32], T.big1[:, 0:1], T.f2[:, 125:128]):
-        v("ms", b, 0.0)
-    zero = v("ms", T.t3[:], 0)
-    v("tr", T.lo_c[:], T.lo_r[:, 0:32], after=[rows])
-    key = v("tr", T.key_c[:], T.key_r[:, 0:32])
-    v("tr", T.q_c[:], T.q_r[:])
-    v("ms", T.win1[:], 0.0)
-    lm = v("ts", T.lm[R, :], T.key_r[R, 0:32], T.key_c[R, 0:1], op.is_gt, after=[key])
-    fill(T.rst, 128, 0, 130, 1.0, after=[ones])
-    full = fill(T.rst8, 32, 0, 192, 1.0)
-    z2 = fill(T.z2, 128, 0, 32, 0.0)
-    c80 = fill(T.c80, 32, 0, 5, float(SLOT))
-    rst = fill(T.rst, 128, 0, 130, 0.0, step=N, after=[full])
-    fill(T.rst8, 32, 0, 192, 0.0, step=G)
-    for buf, tall, c0, c1, value in ((T.bmp, 128, 0, 32, 192.0), (T.cs2, 128, 0, 5, 128.0), (T.tb2, 128, 0, 128, 128.0),
-                                     (T.la3, 32, 0, 32, 0.0), (T.eb3, 32, 0, 32, 0.0),
-                                     (T.val3, 128, 0, 128, 0.0), (T.val3, 128, 128, 256, 0.0), (T.v3, 32, 0, W, 0.0),
-                                     (T.win3, 128, mine, mine + 192, 0.0), (T.win3, 128, mine + 192, mine + COLS, 0.0)):
-        filled = fill(buf, tall, c0, c1, value)
+    def pack(b):
+        return v("qz", T.q[:, 128 * b:128 * b + 128], T.p[:, 128 * b:128 * b + 128], T.xt[:, 512 * b:512 * b + 512], after=[l_x[b]])
 
-    lists = send([(r, own, own) for r in order[:-1]], "sl", [l_own])
-    for a, b, base in ((0, rest, me + 1), (rest, N, 0)):
-        if b > a:
-            f2 = iota(T.f2[0:1, 25 * a:25 * b], [[1, b - a], [0, 5], [N, N]], base, after=[zero])
-    sa0 = sel(T.sa0[:], T.ones[0:32, 0:30], [[-H, 5], [0, H]], op.is_ge, 0, 1)
-    tb0 = iota(T.tb0[:], [[0, 5], [16, 5]], 128)
-    for blk in range(2):
-        for odd in range(2):
-            l_v1 = dma("y", T.val1[16 * odd:128:32, 96 * blk:96 * blk + 96],
-                       T.nat[16 * odd:128:32, :, 32 * blk + 16 * odd:32 * blk + 16 * odd + 16], "d_v1", after=[zero, nat])
+    def pack_w(o):
+        return v("qz", T.wq[:, 128 * o:128 * o + 128], T.wp[:, 128 * o:128 * o + 128], T.wt[:, 512 * o:512 * o + 512], after=[l_w])
+    SIDE, RANK, BACK, KC, NLT, K1, K3, Q12, SEG = [T.col[:, i:i + 1] for i in range(9)]
+    mine, row = COLS * me, T.land[:, 16 + U * me:16 + U * me + U]
+
+    for a in range(NB):
+        l_e1 = dma("y" if a % 2 else "a", T.e[BLK[a], 0:U], T.to[:], "d_e1")
+    l_own = dma("y", T.mine[:], T.to[:], "d_l")
+    l_x = [dma("y", T.xt[:, 512 * b:512 * b + 512], T.x[:, 512 * b:512 * b + 512], "d_x%d" % b) for b in range(3)]
     l_w = dma("y", T.wt[:], T.w[:], "d_w")
 
-    v("ts", T.ab0[R, :], T.e1[R, :], T.lo_c[R, 0:1], op.is_ge, after=[l_e1, lm])
-    t = v("ts", T.ab1[R, :], T.e1[R, :], -float(COLS), op.add, T.lo_c[R, 0:1], op.is_ge)
-    big = v("ts", T.big1[R, 1:65], T.e1[R, :], T.lo_c[R, 0:1], op.is_ge, BIG, op.mult)
-    t = v("scan", T.c1[R, :], T.ab0[R, :], T.ab1[R, :], 0.0, op.add, op.subtract, after=[t])
-    v("ts", T.up1[R, 32:96], T.e1[R, :], T.lo_c[R, 0:1], op.is_ge, BIG + 1, op.mult)
-    t = v("ts", T.ln1[R, :], T.lm[R, :], T.c1[R, W - 1:W], op.mult, after=[t])
-    v("tt", T.dn1[R, 32:96], T.ab1[R, :], T.big1[R, 0:64], op.add, after=[big])
-    t = v("tr", T.up1[:, 0:32], T.ln1[:], after=[t])
-    g1 = v("scan", T.g1[R, :], T.up1[R, :], T.dn1[R, :], 0.0, op.add, op.subtract, after=[t])
-    for a in range(4):
-        bmp = act(T.bmp[32 * a:32 * a + N, :], T.ones[0:N, 0:32], LINE, scale=T.g1[0:N, 31:32], bias=-192.0, after=[filled, g1])
-    for b in range(G):
-        l_z = dma("y", T.z2[32 * (b // 2):32 * (b // 2) + 8, 16 * (b % 2):16 * (b % 2) + 16], T.f2[0:1, :], "d_z", after=[f2, z2])
+    pc = iota(T.pc[:], [[0, 16]], 0, 129)
+    thr = iota(T.thr[:], [[COLS, N + 1], [0, 16]], 0, 0)
+    val1 = iota(T.val1[:], [[16, U], [1, 8], [192, 2]], -248, 1)
+    ones = v("ms", T.ones[:], 1.0)
+    zero = v("ms", T.ge[:], 0.0)
+    pad = v("ms", T.e[:, U:32], -1)
+    low = v("ts", T.ti[:, 0:4], T.pc[:, 0:4], 15, op.bitwise_and, after=[pc])
+    v("ts", T.ti[:, 4:10], T.pc[:, 0:6], 7, op.bitwise_and)
+    t = v("ts", T.ti[:, 10:11], T.pc[:, 0:1], 3, op.logical_shift_right, 0x71, op.bitwise_and)
+    ramp = v("scan", T.ramp[:], T.ones[:, 0:16], T.ones[:, 0:16], -1.0, op.add, op.mult, after=[ones])
+    tu = v("cp", T.tu[:, 0:4], T.ti[:, 0:4], after=[low])
+    qf = v("cp", T.qf[:], T.ti[:, 0:1])
+    seg = v("ts", SEG, T.ti[:, 10:11], 81.0, op.min, after=[t])
+    fill(T.cb[:, 15:544:16], 34, 0.0, after=[ones])
+    fill(T.yy[:, 0:65], 65, 0.0)
+    first = fill(T.ge[:, 0:U], U, 1.0, after=[zero])
+    full = fill(T.rst[:], 128, 1.0)
+    fill(T.fifth[:], 32, 0.2)
+    fill(T.rst[:, 0:128:5], 26, 0.0, after=[full])
+    q12 = act(Q12, T.qf[:], scale=float(U), bias=10.0, after=[qf, ramp])
 
-    def pack(b, after=()):
-        return v("qz", T.q[:, 128 * b:128 * b + 128], T.p[:, 128 * b:128 * b + 128], T.xt[:, 512 * b:512 * b + 512], after=after)
-    t = v("tr", T.zt1[:], T.g1[:, 32:96], after=[g1])
-    pack(0, [l_x])
-    v("scan", T.s1[:, 0:30], T.rst[0:32, 0:30], T.zt1[:, 0:30], 0.0, op.mult, op.max, after=[t, rst])
-    t = v("scan", T.s1[:, 30:60], T.rst[0:32, 0:30], T.zt1[:, 32:62], 0.0, op.mult, op.max)
-    pack(1)
-    for a in range(4):
-        of1 = v("ts", T.of1[32 * a:32 * a + 32, :], T.s1[:, 4:60:5], -1.0 - BIG, op.add, after=[t])
-    rowp = v("tr", T.rowp[:], T.bmp[:], after=[bmp])
-    win1 = v("cp", T.win1[:, 0:400].indirect(T.of1[:, 0:12]), T.val1[:], after=[of1, l_v1])
-    packed = pack(2)
+    lists = send([(r, T.mine[:], T.lists[128 * (NB - 1 - j):128 * (NB - j), :]) for j, r in enumerate(order[:-1])], "sl", [l_own])
+    for a in range(NB):
+        dma("y", T.e[BLK[a], 16 + U:19 + U], T.mine[a:128:NB, :], "d_e3", after=[l_own, pad])
 
-    counts = send([(r, T.rowp[:, 0:8], T.land[:, me, :]) for r in order[:-1]], "sp", [rowp])
-    sam = sel(T.sam[:], T.sa0[:], [[H, 5], [0, H]], op.is_ge, H - 1, -1, after=[sa0])
-    mx0 = sel(T.mx0[:], T.c80[:], [[-H, 5]], op.is_ge, 0, 1, after=[c80])
-    low = sel(T.low[:], T.ones[0:32, 0:5], [[-H, 5]], op.is_ge, -H, 1)
-    sel(T.lsa[:], T.sam[:], [[1, 30]], op.is_gt, 0, -1, after=[sam])
-    sel(T.mx[:], T.mx0[:], [[H, 5]], op.is_ge, H - 1, -1, after=[mx0])
-    tables = iota(T.t80[:], [[SLOT, N], [0, N]])
-    act(T.land[:, me, :], T.rowp[:, 0:8], COPY, after=[rowp])
+    def trl():
+        v("tr", T.yy[:, 32:64], T.cb[:, 15:527:16], after=[k["c1"]])
+        return v("tr", T.yy[:, 65:97], T.cb[:, 31:543:16])
 
-    l_e3 = dma("y", T.e3[R, :], T.lists[:], "d_e3", after=[lists, l_own])
-    for b, a0, a1, row in [(b, 4 * b, min(4 * b + 4, N * H), 0) for b in range(G)] + [(G - 1, 0, 2, 8)]:
-        top = 32 * (b // 2) + row
-        l_t3 = dma("y", T.t3[top:top + 4 * (a1 - a0), 16 * (b % 2):16 * (b % 2) + 16], T.e3[a0:a1, :], "d_t3", after=[l_e3, zero])
+    def counts1():
+        n1 = act(T.n1[:], T.s4[:, 31:32], scale=-1.0, bias=T.s4[:, 64:65], after=[k["s4"]])
+        k["bml"] = act(T.bml[:], T.ones[:, 0:32], scale=T.s4[:, 31:32], bias=-192.0)
+        return act(T.bmc[:], T.fifth[:], scale=T.n1[:], bias=128.4, after=[n1])
+    steps = {
+        "ge": lambda: v("tt", T.ge[:, 16:80], T.e[:, 0:16].indirect(T.tu[:, 0:4]), T.thr[:, 16:80], op.is_ge, after=[l_e1, tu, thr]),
+        "tc": lambda: v("ts", T.tu[:, 10:16], T.ramp[:, 0:6], 2.0, op.mult, SEG, op.add, after=[seg]),
+        "c1": lambda: v("scan", T.cb[:, 16:112], T.ge[:, 0:96], T.ge[:, 16:112], 0.0, op.add, op.subtract, after=[k["ge"], first]),
+        "xs": lambda: act(T.xs[:], T.ge[:].indirect(T.tu[:, 10:16]), COPY, scale=STEP, after=[k["ge"], k["tc"], first]),
+        "cg": lambda: v("cp", T.cg[:], T.cb[:, 16:112].indirect(T.tu[:, 10:16]), after=[k["c1"], k["tc"]]),
+        "jz": lambda: act(T.jz[:], T.ramp[:, 0:8], scale=16.0 * U, bias=Q12, after=[q12]),
+        "p96": lambda: v("ts", T.ti[:, 11:12], T.pc[:, 0:1], 96, op.bitwise_and),
+        "tu8": lambda: v("cp", T.tu[:, 4:10], T.ti[:, 4:10]),
+        "trl": trl, "counts1": counts1,
+        "win0": lambda: [act(T.win1[:, c:c + n], T.val1[:, 0:n], COPY, scale=0.0, after=[val1]) for c, n in ((0, 192), (192, 192), (384, 16))][-1],
+        "s4": lambda: v("scan", T.s4[:], T.yy[:, 32:97], T.yy[:, 0:65], 0.0, op.add, op.subtract, after=[k["trl"]]),
+        "back": lambda: v("ts", BACK, T.ti[:, 11:12], -1.0, op.mult, 240.0, op.add, after=[k["p96"]]),
+        "base": lambda: v("tr", T.bt[:], T.s4[:, 32:64], after=[k["s4"]]),
+        "cand": lambda: v("tt", T.cand[:], T.bt[:].indirect(T.tu[:, 4:10]), T.cg[:], op.add, after=[k["base"], k["cg"], k["tu8"]]),
+        "order": lambda: v("scan", T.sc[:], T.xs[:], T.cand[:], 0.0, op.max, op.min, after=[k["cand"], k["xs"]]),
+        "rowl": lambda: v("tr", T.rowp[:, 0:32], T.bml[:], after=[k["bml"]]),
+        "rowc": lambda: v("tr", T.rowp[:, 6:38], T.bmc[:], after=[k["counts1"], k["rowl"]]),
+        "of1": lambda: v("ts", T.of1[:], T.sc[:, 4:96:8], -1.0, op.add, after=[k["order"]]),
+        "win1": lambda: v("cp", T.win1[:].indirect(T.of1[:]), T.val1[:], after=[k["of1"], k["win0"], val1]),
+        "counts": lambda: send([(r, T.rowp[:, 0:U], row) for r in order[:-1]], "sp", [k["rowc"]]),
+        "x0": lambda: pack(0), "x1": lambda: pack(1),
+    }
+    for name in FIRST.split():
+        k[name] = steps[name]()
+    rowp, counts, win1, back, sc = k["rowc"], k["counts"], k["win1"], k["back"], k["order"]
+    l_o = dma("y", row, T.rowp[:, 0:U], "d_o", after=[rowp])
+    l_e3 = dma("y", T.e[:, 16:16 + U], T.lists[:], "d_e3", after=[lists])
 
-    for i, k in enumerate(order):
+    iota(T.tb2[:], [[0, 128]], 128, 0)
+    tb0 = iota(T.tb0[:], [[0, N], [16, 5]], 128, 0)
+    iota(T.z[:], [[0, 64]], 0, 0)
+    iota(T.land[:, 0:16], [[0, 16]], 128, 0)
+    t80 = iota(T.t80[:], [[SLOT, N + 1], [0, U]], -129 - SLOT, 0)
+    side = act(SIDE, T.qf[:], FN.Sign, bias=0.5 - U)
+    ja = act(T.ja[:], T.jz[:], scale=0.2 / U, bias=128.6 - 2.0 / U, after=[k["jz"]])
+    for a in range(NB):
+        rank = act(T.col[BLK[a], 1:2], T.col[BLK[a], 0:1], scale=(me - order[a]) / 2, bias=(me + order[a]) / 2, after=[side])
+    jt = act(T.jt[:], T.ja[:], scale=0.2 - 5 * U, bias=129 * (5 * U - 0.2) - 0.4, after=[ja])
+    nlt = act(NLT, T.rowp[:, me:me + 1], scale=-1.0, bias=-192.0, after=[rowp])
+
+    def turn(i):
         for u in (0, 16):
-            out, in_ = T.dup1[:, 5 * i:5 * i + 5, u:u + 16], T.win1[:, k:400:5]
-            if i < 3:
-                t = v("cp", out, in_, after=[win1])
-            else:
-                dup = act(out, in_, COPY, after=[win1])
-    t = v("tr", T.tr1[:], T.dup1[:], after=[t, dup])
-    t = v("tt", T.sm1[:], T.tr1[:, 0:800:32], T.tr1[:, 16:800:32], op.add, after=[t])
-    l1 = v("ts", T.l1[:, 0:25], T.sm1[:], 192.0, op.add, after=[t])
+            out, in_ = T.dup1[:, 5 * i:5 * i + 5, u:u + 16], T.win1[:, order[i]:400:5]
+            t = v("cp", out, in_, after=[win1]) if i in (2, 3) else act(out, in_, COPY, after=[win1])
+        if i == NB:
+            k["tb2"] = act(T.tb2[:, 0:125:5], T.tb0[:], bias=T.qf[:], after=[tb0])
+        return t
 
-    def hop(cw, pw, lst, co, po, cl, pl, n, sc, sp, for_codes, for_planes, between=None):
-        u8 = lambda a: a.bitcast(dt.uint8)
-        for i in range(2):
-            kc = codes(co[:, 160 * i:160 * i + 160], cw, lst[:, 10 * i:10 * i + 10], for_codes)
-            kp = planes(po[:, 160 * i:160 * i + 160], pw, lst[:, 10 * i:10 * i + 10], for_planes)
-            if between and i == 0:
-                between()
-            come = send([(order[j], u8(co[:, cut(j, n)]), u8(cl[:, cut(me, n)])) for j in (2 * i, 2 * i + 1)], sc, [kc])
-        return come, send([(r, po[:, cut(j, n)], pl[:, cut(me, n)]) for j, r in enumerate(order[:-1])], sp, [kp])
+    def list1(step, i0, i1, after):
+        if step == 0:
+            return v("tr", T.tr1[:, 160 * i0:160 * i1], T.dup1[:, 5 * i0:5 * i1, :], after=after)
+        if step == 1:
+            return v("tt", T.sm1[:, 5 * i0:5 * i1], T.tr1[:, 160 * i0 + 8:160 * i1:32], T.tr1[:, 160 * i0 + 16:160 * i1:32], op.add, after=after)
+        return v("ts", T.l1[:, 5 * i0:5 * i1], T.sm1[:, 5 * i0:5 * i1], BACK, op.add, after=after)
 
-    c1, p1 = hop(T.q, T.p, T.l1, T.q2, T.p2, T.ql, T.pl, SENT1, "s1c", "s1p", [l1], [l1, packed])
+    def ge3():
+        return v("tt", T.ea[:], T.e[:, 16:32].indirect(T.tu[:, 0:2]), T.thr[:, 16 * me:16 * me + 32], op.is_ge, after=[l_e3, t80])
 
-    v("ts", T.ea3[R, 32:96], T.e3[R, :], float(mine), op.is_ge, after=[l_e3])
-    a3 = v("ts", T.eb3[R, 32:96], T.e3[R, :], float(mine + COLS), op.is_ge)
-    zc = v("tr", T.zc2[:], T.z2[:], after=[l_z])
-    nn = v("tt", T.nn2[:], T.land[:, :, 1:6], T.land[:, :, 0:5], op.subtract, after=[counts])
-    xa = v("tt", T.xo3[R, 0:5], T.land[R, :, me], T.mx[R, :], op.mult, after=[tables])
-    tb2 = act(T.tb2[:, 0:125:5], T.tb0[:], LINE, bias=T.q_c[:, 0:1], after=[tb0])
-    act(T.jk3[R, 15:20], T.low[R, :], LINE, scale=-128.0, bias=3016.0, accum_out=T.gb3[R, 0:1], after=[tables])
-    own_p1 = planes(T.pl[:, cut(me, SLOT)], T.p, T.l1[:, 20:25])
-    cp = act(T.jk3[R, 0:5], T.xo3[R, 0:5], LINE, scale=0.0025, bias=7.56, accum_out=T.cp3[R, 0:1], after=[xa])
-    a3 = v("scan", T.c3[R, :], T.ea3[R, 32:96], T.eb3[R, 32:96], 0.0, op.add, op.subtract, after=[a3])
-    of2 = v("cp", T.of2[:], T.zc2[:, 0:8], after=[zc])
-    cs = v("ts", T.cs2[:, 5:30], T.nn2[:], 0.2, op.mult, 128.4, op.add, after=[nn])
-    ci = v("ts", T.ci0[:], T.land[:, :, 0:5], 0.2, op.mult, 38.8 - 0.2 * me, op.add)
-    a3 = v("ts", T.la3[R, 0:30], T.lsa[R, :], T.c3[R, W - 1:W], op.mult, after=[a3])
-    xb = v("tt", T.xo3[R, 5:10], T.cs2[R, 5 + me:30:5], T.low[R, :], op.mult, after=[cs])
-    b2 = v("tt", T.d2[:], T.cs2[:, 0:30].indirect(T.of2[:]), T.tb2[:], op.subtract, after=[of2, tb2])
-    cv = act(T.jk3[R, 5:15], T.xo3[R, :], LINE, accum_out=T.cv3[R, 0:1], after=[xb])
-    a3 = v("tr", T.ea3[:, 0:32], T.la3[:], after=[a3])
-    ci = v("tt", T.ci2[:, 0:25], T.ci0[:], T.t80[:], op.add, after=[ci])
-    u2 = v("scan", T.u2[:], T.rst[:, 0:128], T.d2[:], 0.0, op.mult, op.add, after=[b2])
-    gx = act(T.gx2[:], T.u2[:], LINE, scale=-STEP, bias=STEP / 2, after=[u2])
-    g3 = v("scan", T.g3[R, :], T.ea3[R, :], T.eb3[R, :], 0.0, op.add, op.subtract, after=[a3])
-    gv = act(T.gv3[R, :], T.g3[R, 32:96], LINE, scale=float(SLOT), bias=T.gb3[R, 0:1], after=[g3, cp])
-    b2 = v("tt", T.fx2[:], T.ci2[:, 0:25].indirect(T.of2[:]), T.u2[:], op.subtract, after=[u2, ci])
-    v("ts", T.pp3[R, :], T.g3[R, 32:96], 0.2, op.mult, T.cp3[R, 0:1], op.add, after=[g3, cp])
-    a3 = v("ts", T.qq3[R, :], T.g3[R, 32:96], 0.2, op.mult, -0.6, op.add)
-    b2 = v("scan", T.ss2[:], T.gx2[:, 0:125], T.fx2[:, 0:125], 0.0, op.max, op.min, after=[b2, gx])
-    v("ts", T.tp3[R, :], T.pp3[R, :], -400.0, op.mult, T.cv3[R, 0:1], op.add, after=[a3, cv])
-    a3 = v("tt", T.ts3[R, :], T.gv3[R, :], T.qq3[R, :], op.add, after=[gv])
-    l2 = v("ts", T.l2[:, 0:25], T.ss2[:, 4:125:5], float(SLOT * (N - 1) + SENT1 - 1), op.min, after=[b2])
-    own_c1 = codes(T.ql[:, cut(me, SLOT)], T.q, T.l1[:, 20:25])
-    v3 = v("tt", T.v3[R, :], T.tp3[R, :], T.ts3[R, :], op.add, after=[a3])
-    l_v3 = dma("y", T.val3[0:128:16, :], T.v3[:], "d_v3", after=[v3, filled])
-    at = {"t": v("cp", T.tf3[:], T.t3[:], after=[l_t3])}
+    def l1c():
+        t = list1(2, 4, 5, [k["sumc"], back])
+        k["ownp1"] = planes(T.pl[:, cut(me, SLOT)], T.p, T.l1[:, 20:25], [t])
+        return t
 
-    def between():
-        at["t"] = v("tr", T.tr0[:], T.tf3[:], after=[at["t"]])
-    c2, p2 = hop(T.ql, T.pl, T.l2, T.q3, T.p3, T.qm, T.pm, SLOT, "s2c", "s2p", [l2, own_c1, c1], [l2, own_p1, p1], between)
-    own_p2 = planes(T.pm[:, cut(me, SLOT)], T.pl, T.l2[:, 20:25])
+    def codes1(i):
+        t = codes(T.q2[:, 160 * i:160 * i + 160], T.q, T.l1[:, 10 * i:10 * i + 10], [k["l1" + "ab"[i]], k["x2"]])
+        return send([(order[j], u8(T.q2[:, cut(j, SENT1)]), u8(T.ql[:, cut(me, SENT1)])) for j in (2 * i, 2 * i + 1)], "s1c", [t])
 
-    of3 = v("cp", T.of3[:], T.tr0[:, 0:16], after=[at["t"]])
-    codes(T.qm[:, cut(me, SLOT)], T.ql, T.l2[:, 20:25])
-    win3 = v("cp", T.win3[:].indirect(T.of3[:]), T.val3[:], after=[of3, l_v3])
-    v("qz", T.wq[:, 0:128], T.wp[:, 0:128], T.wt[:, 0:512], after=[l_w])
-    dup = act(T.dup3[:, 12:24, 16:32], T.win3[:, mine + 192:mine + 384], COPY, after=[win3])
-    v("cp", T.dup3[:, :, 0:16], T.win3[:, mine:mine + 384], after=[win3])
-    t = v("cp", T.dup3[:, 0:12, 16:32], T.win3[:, mine:mine + 192])
-    wq = v("qz", T.wq[:, 128:256], T.wp[:, 128:256], T.wt[:, 512:1024])
-    tr3 = v("tr", T.tr3[:], T.dup3[:], after=[t, dup])
-    for r in range(G):
-        out, in_ = T.su3[:, r:192:G], T.tr3[32 * (r // 2):32 * (r // 2) + 32, 16 * (r % 2):768:32]
-        if r < G // 2:
-            t = v("cp", out, in_, after=[tr3])
-        else:
-            su = act(out, in_, COPY, after=[tr3])
-    t = v("scan", T.sv3[:], T.rst8[:], T.su3[:], 0.0, op.mult, op.add, after=[t, su])
-    for a in range(4):
-        l3 = v("ts", T.l3[32 * a:32 * a + 32, :], T.sv3[:, G - 1:192:G], 200.0, op.add, after=[t])
+    def planes1():
+        for a in range(NB):
+            own = act(T.z[BLK[a], U:U + 3], T.sc[BLK[a], 24 * a + 4:24 * a + 24:8], bias=T.col[BLK[a], 4:5], after=[nlt, sc, t80])
+        planes(T.p2[:, 160:320], T.p, T.l1[:, 10:20], [k["l1b"], k["x2"]])
+        k["own"] = act(T.z[:, 32 + U:35 + U], T.z[:, U:U + 3], COPY, after=[own])
+        pa = planes(T.p2[:, 0:160], T.p, T.l1[:, 0:10], [k["l1a"]])
+        k["ci0"] = act(T.ci0[:], T.land[:, 6:76], scale=0.2, bias=167.8 - 0.2 * me, after=[counts, l_o])
+        k["kc"] = act(KC, RANK, scale=-128.0, bias=SLOT * (209 + me) - 200.6)
+        return send([(r, T.p2[:, cut(j, SENT1)], T.pl[:, cut(me, SENT1)]) for j, r in enumerate(order[:-1])], "s1p", [pa])
 
-    wait("m", [wq, own_p2, c2, p2])
-    res, copied, part = (T.rs0, T.rs1), [], N * SLOT // 2
-    for b in range(4):
-        o, c, bank = b // 2, slice(part * (b % 2), part * (b % 2) + part), T.ps[:, 512 * b:512 * b + part]
-        t = mark(g.tensor.matmul_mx(bank, T.wq[:, 128 * o:128 * o + 128], T.wp[:, 128 * o:128 * o + 128],
-                                    T.qm[:, c], T.pm[:, c], True, True), "m", 1)
-        copied.append(act(res[o][:, c], bank, COPY, after=[t]) if b % 2 else v("cp", res[o][:, c], bank, after=[t]))
-    HALF = COLS // 2
-    for h in range(2):
+    def u2():
+        t = v("scan", T.u2[:], T.rst[:], T.d2[:], 0.0, op.mult, op.add, after=[k["d2"]])
+        k["gx"] = act(T.gx2[:], T.u2[:], scale=-STEP, bias=STEP / 2, after=[t])
+        return t
+
+    def rows():
+        return v("ms", T.win3[:, mine:mine + COLS], 0.0)
+
+    def xo():
+        t = v("tt", T.xo[:], T.land[:, 16 + me:76:6], T.sel[:], op.mult, after=[k["is"], k["below"], counts, l_o])
+        k["k1"] = act(T.jk[:, 0:5], T.xo[:, 0:10:2], scale=0.0025, bias=(0.2 * (209 + me) - 0.4) / 5, accum_out=K1, after=[t])
+        return act(T.jk[:, 5:15], T.xo[:], accum_out=K3)
+
+    def l2():
+        for a, b, d in ((0, rest, me + 1), (rest, N, 0)):
+            if b > a:
+                t = v("ts", T.l2[:, 5 * a:5 * b], T.ss2[:, 25 * d + 4:25 * (d + b - a):5], float(SLOT * (N - 1) + SENT1 - 1), op.min, after=[k["ss2"]])
+        return t
+
+    def planes2():
+        need = [k["l2"], k["ownp1"], k["planes1"]]
+        pb = planes(T.p3[:, 160:320], T.pl, T.l2[:, 10:20], need)
+        pa = v("cp", T.p3[:, 0:160], T.pl[:].indirect(T.l2[:, 0:10]), after=need)
+        k["ownp2"] = planes(T.pm[:, cut(0, SLOT)], T.pl, T.l2[:, 20:25])
+        for c in (0, 96):
+            full = act(T.rst8[:, c:c + 96], T.ones[0:32, 0:96], COPY)
+        k["rst8"] = act(T.rst8[:, 0:192:8], T.ones[0:32, 0:24], COPY, scale=0.0, after=[full])
+        return send([(r, T.p3[:, cut(j, SLOT)], T.pm[:, cut(j + 1, SLOT)]) for j, r in enumerate(order[:-1])], "s2p", [pa, pb])
+
+    def codes2(i):
+        t = codes(T.q3[:, 160 * i:160 * i + 160], T.ql, T.l2[:, 10 * i:10 * i + 10], [k["l2"], k["own1"], k["codes1a"]])
+        return send([(order[j], u8(T.q3[:, cut(j, SLOT)]), u8(T.qm[:, cut(j + 1, SLOT)])) for j in (2 * i, 2 * i + 1)], ("s2a", "s2b")[i], [t])
+
+    def v3():
+        t = v("tt", T.v3[:], T.b3[:], T.tp3[:], op.add, after=[k["b3"], k["tp3"]])
+        for h in range(2):
+            k["val3"] = dma("y", T.val3[16 * h:128:32, :], T.v3[:, 16 * h:16 * h + 16], "d_v3", after=[t, k["val0"]])
+
+    def wide():
+        k["wide2"] = act(T.dup3[:, 12:24, 16:32], T.win3[:, mine + 192:mine + COLS], COPY, after=[k["win3"]])
+        v("cp", T.dup3[:, :, 0:16], T.win3[:, mine:mine + COLS], after=[k["win3"]])
+        return v("cp", T.dup3[:, 0:12, 16:32], T.win3[:, mine:mine + 192])
+
+    def blocks():
+        for r in range(8):
+            out, in_ = T.su3[:, r:192:8], T.tr3[BLK[r // 2], 16 * (r % 2):768:32]
+            k["su%d" % (r // 6)] = act(out, in_, COPY, after=[k["trw"]]) if r // 6 else v("cp", out, in_, after=[k["trw"]])
+
+    def l3():
+        for a in range(NB):
+            t = v("ts", T.l3[BLK[a], :], T.sw3[:, 7:192:8], 200.0, op.add, after=[k["sum8"]])
+        return t
+    steps = {
+        "jw": lambda: v("tt", T.jw[:], T.jz[:], T.jt[:], op.add, after=[jt]),
+        "of2": lambda: v("cp", T.of2[:], T.jw[:], after=[k["jw"]]),
+        "tra": lambda: list1(0, 0, 2, [k["turn1"]]), "suma": lambda: list1(1, 0, 2, [k["tra"]]), "l1a": lambda: list1(2, 0, 2, [k["suma"], back]),
+        "trb": lambda: list1(0, 2, 4, [k["turn3"]]), "sumb": lambda: list1(1, 2, 4, [k["trb"]]), "l1b": lambda: list1(2, 2, 4, [k["sumb"], back]),
+        "trc": lambda: list1(0, 4, 5, [k["turn4"]]), "sumc": lambda: list1(1, 4, 5, [k["trc"]]), "l1c": l1c,
+        "planes1": planes1, "codes1a": lambda: codes1(0), "codes1b": lambda: codes1(1),
+        "own1": lambda: codes(T.ql[:, cut(me, SLOT)], T.q, T.l1[:, 20:25], [k["l1c"]]),
+        "d2": lambda: v("tt", T.d2[:], T.land[:, 0:76].indirect(T.of2[:]), T.tb2[:], op.subtract, after=[k["of2"], k["tb2"], t80, counts, l_o]),
+        "u2": u2, "ci2": lambda: v("tt", T.ci2[:], T.ci0[:], T.t80[:, 2:72], op.add, after=[k["ci0"], t80]),
+        "fx2": lambda: v("tt", T.fx2[:], T.ci2[:].indirect(T.of2[:]), T.u2[:], op.subtract, after=[k["u2"], k["ci2"]]),
+        "ss2": lambda: v("scan", T.ss2[:], T.gx2[:, 0:125], T.fx2[:, 0:125], 0.0, op.max, op.min, after=[k["fx2"], k["gx"]]),
+        "l2": l2, "planes2": planes2, "codes2a": lambda: codes2(0), "codes2b": lambda: codes2(1),
+        "own2": lambda: codes(T.qm[:, cut(0, SLOT)], T.ql, T.l2[:, 20:25]),
+        "is": lambda: v("ts", T.sel[:, 0:10:2], T.ramp[:, 0:N], RANK, op.is_equal, -float(SLOT), op.mult, after=[rank]),
+        "below": lambda: v("ts", T.sel[:, 1:10:2], T.ramp[:, 0:N], RANK, op.is_lt, after=[rank]),
+        "val0": lambda: v("ms", T.val3[:, 0:240], 0.0), "ge3": ge3, "rows": rows, "xo": xo, "v3": v3,
+        "scan3": lambda: v("scan", T.z[:, 32:32 + U], T.ea[:, 0:U], T.ea[:, 16:16 + U], 0.0, op.add, op.subtract, after=[k["ge3"]]),
+        "rest3": lambda: v("ts", T.z[:, 0:U], T.z[:, 32:32 + U], T.z[:, 31 + U:32 + U], op.subtract, after=[k["scan3"]]),
+        "tr3": lambda: v("tr", T.yy[:, 32:96], T.z[:], after=[k["rest3"], k["own"]]),
+        "m3": lambda: v("scan", T.m3[:], T.yy[:, 64:96], T.yy[:, 31:63], 0.0, op.add, op.subtract, after=[k["tr3"]]),
+        "b3": lambda: v("ts", T.b3[:], T.m3[:], 0.2 - SLOT, op.mult, KC, op.add, after=[k["m3"], k["kc"]]),
+        "a3": lambda: v("ts", T.a3[:], T.m3[:], -0.2, op.mult, K1, op.add, after=[k["m3"], k["k1"]]),
+        "tp3": lambda: v("ts", T.tp3[:], T.a3[:], -5.0 * SLOT, op.mult, K3, op.add, after=[k["a3"], k["xo"]]),
+        "of3": lambda: v("cp", T.of3[:, 0:15], T.e[:, 16:31], after=[l_e3]),
+        "win3": lambda: v("cp", T.win3[:].indirect(T.of3[:, 0:15]), T.val3[:, 0:240], after=[k["of3"], k["val3"], k["rows"]]),
+        "wide": wide, "trw": lambda: v("tr", T.tr3[:], T.dup3[:], after=[k["wide"], k["wide2"]]),
+        "blocks": blocks,
+        "sum8": lambda: v("scan", T.sw3[:], T.rst8[:], T.su3[:], 0.0, op.mult, op.add, after=[k["su0"], k["su1"], k["rst8"]]),
+        "l3": l3, "x2": lambda: pack(2), "w0": lambda: pack_w(0), "w1": lambda: pack_w(1),
+    }
+    steps.update({"turn%d" % i: lambda i=i: turn(i) for i in range(N)})
+    for name in ORDER.split():
+        k[name] = steps[name]()
+
+    res, copied = (T.rs0, T.rs1), []
+    for b, c in enumerate((slice(0, 3 * SLOT), slice(3 * SLOT, N * SLOT))):
+        wait("m", [k["w0"], k["w1"], k["own2"], k["ownp2"], k["planes2"], k["codes2" + "ab"[b]]])
         for o in range(2):
-            c = slice(COLS * o + HALF * h, COLS * o + HALF * h + HALF)
-            pick, need = res[o][:].indirect(T.l3[:, 12 * h:12 * h + 12]), copied[2 * o:2 * o + 2] + [l3]
-            t = act(T.ys[:, c], pick, COPY, after=need) if o else v("cp", T.ys[:, c], pick, after=need)
-            if o and h:
-                wait("a", [dma("a", T.y[:, c], T.ys[:, c], "st2", after=[t])])
-            else:
-                stored = dma("y", T.y[:, c], T.ys[:, c], "st", after=[t])
+            bank = T.ps[:, 512 * (2 * b + o):512 * (2 * b + o) + c.stop - c.start]
+            t = mark(g.tensor.matmul_mx(bank, T.wq[:, 128 * o:128 * o + 128], T.wp[:, 128 * o:128 * o + 128],
+                                        T.qm[:, c], T.pm[:, c], True, True), "m", 1)
+            copied.append(act(res[o][:, c], bank, COPY, after=[t]))
+    for n, (q, o, a, b) in enumerate(PIECES):
+        c = slice(COLS * o + 16 * a, COLS * o + 16 * b)
+        pick, need = res[o][:].indirect(T.l3[:, a:b]), [copied[o], copied[2 + o], k["l3"]]
+        t = act(T.ys[:, c], pick, COPY, after=need) if q == "a" else v("cp", T.ys[:, c], pick, after=need)
+        if n < len(PIECES) - 1:
+            stored = dma("y", T.y[:, c], T.ys[:, c], "st", after=[t])
+        else:
+            wait("a", [dma("a", T.y[:, c], T.ys[:, c], "st2", after=[t])])
     wait("y", [stored])
-    wait("g", [(s, count[s]) for s in ("v", "g", "loc")])
+    wait("g", [(s, count[s]) for s in ("v", "a", "g", "loc")])

from concourse.bass import DstId, RemoteDMATransfer
from concourse.mybir import dt, AluOpType, ActivationFunctionType

N, COLS = 5, 384
SLOT = 80
SENT1 = 78
U = 12
STEP = 1024.0
NB = N - 1

F32, BF, I32, U16 = "float32", "bfloat16", "int32", "uint16"
X4, U8 = "float8_e4m3fn_x4", "uint8"
SMALL = {
    X4: "q:128,384 wq:128,256 q2:128,320 ql:128,400 q3:128,320 qm:128,400",
    U8: "p:128,384 wp:128,256 p2:128,320 pl:128,400 p3:128,320 pm:128,400",
    BF: "xt:128,1536 wt:128,1024 val1:128,192 win1:128,400 dup1:128,25,32 tr1:128,800 bml:128,32 bmc:128,32 rowp:128,48 "
        "land:128,80 ci0:128,70 ja:128,8 v3:128,32 val3:128,512 win3:128,1920 dup3:128,24,32 "
        "tr3:128,768 su3:32,192 rst8:32,192 sw3:32,192",
    I32: "e:128,32 pc:128,16 ti:128,16 jw:128,8 a3:128,32 b3:128,32",
    U16: "tu:128,16 of1:128,12 l1:128,26 of2:128,8 l2:128,26 of3:128,16 l3:128,24",
    F32: "ys:128,768 rs0:128,400 rs1:128,400 ones:128,128 ramp:128,16 fifth:128,32 thr:128,96 ge:128,112 cb:128,544 yy:128,97 "
         "s4:128,65 bt:128,32 xs:128,96 cg:128,96 cand:128,96 sc:128,96 n1:128,1 sm1:128,25 qf:128,1 "
         "col:128,16 jz:128,8 jt:128,8 rst:128,128 tb0:128,25 tb2:128,128 t80:128,72 ci2:128,70 d2:128,128 u2:128,128 "
         "gx2:128,128 fx2:128,128 ss2:128,125 sel:128,10 xo:128,10 jk:128,16 ea:128,32 z:128,64 m3:128,32 "
         "tp3:128,32",
}
SCRATCH = {"ps": ("psum", [128, 2048], F32), "mine": ("dram", [128, 3], I32), "lists": ("dram", [NB * 128, 3], I32)}
for _t in SMALL:
    for _b in SMALL[_t].split():
        SCRATCH[_b.split(":")[0]] = ("sbuf", [int(_n) for _n in _b.split(":")[1].split(",")], _t)
SEMAPHORES = ["v", "a", "g", "m", "d_e1", "d_x0", "d_x1", "d_x2", "d_w", "d_l", "d_e3", "d_o", "d_v3",
              "sl", "sp", "s1c", "s1p", "s2a", "s2b", "s2p", "loc", "st", "st2"]

FIRST = """ge tc c1 xs win0 p96 trl cg s4 tu8 counts1 jz base back cand x0 order rowl of1 rowc x1 win1 counts"""
ORDER = """x2 turn2 turn3 turn0 turn1 turn4 jw trb of2 sumb tra l1b suma codes1b l1a ge3 trc planes1 d2 scan3 codes1a
rest3 is below u2 tr3 xo ci2 sumc m3 fx2 a3 b3 l1c ss2 tp3 val0 v3 l2 own1 planes2 rows of3
codes2a codes2b win3 own2 w0 wide w1 trw blocks sum8 l3"""
PIECES = (("v", 0, 0, 8), ("a", 1, 0, 10), ("v", 0, 8, 24), ("a", 1, 10, 24))


def cut(r, n):
    return slice(SLOT * r, SLOT * r + n)


def rank_program(g, core, T, topo):
    me = T.rank_of(core)
    if me is None:
        return
    S, V, A, Y = T.sem, g.vector, g.scalar, g.sync
    op, FN = AluOpType, ActivationFunctionType
    COPY, LINE = FN.Copy, FN.Identity
    order = [(me + 1 + i) % N for i in range(N)]
    rest = N - 1 - me
    far = topo.engines(core, T.cores[order[0]])
    queues = {"v": V, "a": A, "g": g, "y": Y, "m": g.tensor}
    count, seen, k = {}, {}, {}
    CALL = {"ts": V.tensor_scalar, "tt": V.tensor_tensor, "cp": V.tensor_copy, "ms": V.memset,
            "scan": V.tensor_tensor_scan, "tr": V.transpose, "qz": V.quantize_mx}
    BLK = [slice(32 * a, 32 * a + 32) for a in range(NB)]

    def wait(q, marks):
        for sem, n in marks:
            if seen.get((q, sem), 0) < n:
                queues[q].wait_ge(S[sem], n)
                seen[q, sem] = n

    def mark(call, sem, n):
        call.then_inc(S[sem], n)
        count[sem] = count.get(sem, 0) + n
        return sem, count[sem]

    def v(name, *args, after=()):
        wait("v", after)
        if name == "ts":
            out, a, s1, o1 = args[:4]
            args = (out, a, s1, None, o1) if len(args) == 4 else (out, a, s1, args[4], o1, args[5])
        return mark(CALL[name](*args), "v", 1)

    def act(out, in_, func=LINE, after=(), **kw):
        wait("a", after)
        return mark(A.activation(out, in_, func, **kw), "a", 1)

    def fill(out, n, value, after=()):
        return act(out, T.ones[:, 0:n], COPY, scale=value, after=after)

    def iota(out, pattern, base, cm):
        return mark(g.iota(out, pattern, base, cm, allow_small_or_imprecise_dtypes=True), "g", 1)

    def dma(q, out, in_, sem, after=()):
        wait(q, after)
        return mark(queues[q].dma_start(out, in_), sem, 16)

    def codes(out, win, off, after=()):
        return v("cp", out.bitcast(dt.uint32), win[:].bitcast(dt.uint32).indirect(off), after=after)

    def planes(out, win, off, after=()):
        return act(out, win[:].indirect(off), COPY, after=after)

    def send(moves, sem, after):
        wait("g", after)
        per, out = len(far) // len(moves), []
        for i, (r, src, dst) in enumerate(moves):
            rid, pid, _ = topo.addr(T.cores[r])
            out.append(RemoteDMATransfer(dst_ids=[DstId(rid=rid, pnc=pid)], dma_engine_mask=sum(1 << b for b in far[per * i:per * i + per]),
                                         remote_sem=S[sem], srcs=[src], dsts=[dst]))
        g.remote_dma_fused(out, local_sem=S.loc)
        for s in (sem, "loc"):
            count[s] = count.get(s, 0) + len(far)
        return sem, count[sem]

    def u8(a):
        return a.bitcast(dt.uint8)

    def pack(b):
        return v("qz", T.q[:, 128 * b:128 * b + 128], T.p[:, 128 * b:128 * b + 128], T.xt[:, 512 * b:512 * b + 512], after=[l_x[b]])

    def pack_w(o):
        return v("qz", T.wq[:, 128 * o:128 * o + 128], T.wp[:, 128 * o:128 * o + 128], T.wt[:, 512 * o:512 * o + 512], after=[l_w])
    SIDE, RANK, BACK, KC, NLT, K1, K3, Q12, SEG = [T.col[:, i:i + 1] for i in range(9)]
    mine, row = COLS * me, T.land[:, 16 + U * me:16 + U * me + U]

    for a in range(NB):
        l_e1 = dma("y" if a % 2 else "a", T.e[BLK[a], 0:U], T.to[:], "d_e1")
    l_own = dma("y", T.mine[:], T.to[:], "d_l")
    l_x = [dma("y", T.xt[:, 512 * b:512 * b + 512], T.x[:, 512 * b:512 * b + 512], "d_x%d" % b) for b in range(3)]
    l_w = dma("y", T.wt[:], T.w[:], "d_w")

    pc = iota(T.pc[:], [[0, 16]], 0, 129)
    thr = iota(T.thr[:], [[COLS, N + 1], [0, 16]], 0, 0)
    val1 = iota(T.val1[:], [[16, U], [1, 8], [192, 2]], -248, 1)
    ones = v("ms", T.ones[:], 1.0)
    zero = v("ms", T.ge[:], 0.0)
    pad = v("ms", T.e[:, U:32], -1)
    low = v("ts", T.ti[:, 0:4], T.pc[:, 0:4], 15, op.bitwise_and, after=[pc])
    v("ts", T.ti[:, 4:10], T.pc[:, 0:6], 7, op.bitwise_and)
    t = v("ts", T.ti[:, 10:11], T.pc[:, 0:1], 3, op.logical_shift_right, 0x71, op.bitwise_and)
    ramp = v("scan", T.ramp[:], T.ones[:, 0:16], T.ones[:, 0:16], -1.0, op.add, op.mult, after=[ones])
    tu = v("cp", T.tu[:, 0:4], T.ti[:, 0:4], after=[low])
    qf = v("cp", T.qf[:], T.ti[:, 0:1])
    seg = v("ts", SEG, T.ti[:, 10:11], 81.0, op.min, after=[t])
    fill(T.cb[:, 15:544:16], 34, 0.0, after=[ones])
    fill(T.yy[:, 0:65], 65, 0.0)
    first = fill(T.ge[:, 0:U], U, 1.0, after=[zero])
    full = fill(T.rst[:], 128, 1.0)
    fill(T.fifth[:], 32, 0.2)
    fill(T.rst[:, 0:128:5], 26, 0.0, after=[full])
    q12 = act(Q12, T.qf[:], scale=float(U), bias=10.0, after=[qf, ramp])

    lists = send([(r, T.mine[:], T.lists[128 * (NB - 1 - j):128 * (NB - j), :]) for j, r in enumerate(order[:-1])], "sl", [l_own])
    for a in range(NB):
        dma("y", T.e[BLK[a], 16 + U:19 + U], T.mine[a:128:NB, :], "d_e3", after=[l_own, pad])

    def trl():
        v("tr", T.yy[:, 32:64], T.cb[:, 15:527:16], after=[k["c1"]])
        return v("tr", T.yy[:, 65:97], T.cb[:, 31:543:16])

    def counts1():
        n1 = act(T.n1[:], T.s4[:, 31:32], scale=-1.0, bias=T.s4[:, 64:65], after=[k["s4"]])
        k["bml"] = act(T.bml[:], T.ones[:, 0:32], scale=T.s4[:, 31:32], bias=-192.0)
        return act(T.bmc[:], T.fifth[:], scale=T.n1[:], bias=128.4, after=[n1])
    steps = {
        "ge": lambda: v("tt", T.ge[:, 16:80], T.e[:, 0:16].indirect(T.tu[:, 0:4]), T.thr[:, 16:80], op.is_ge, after=[l_e1, tu, thr]),
        "tc": lambda: v("ts", T.tu[:, 10:16], T.ramp[:, 0:6], 2.0, op.mult, SEG, op.add, after=[seg]),
        "c1": lambda: v("scan", T.cb[:, 16:112], T.ge[:, 0:96], T.ge[:, 16:112], 0.0, op.add, op.subtract, after=[k["ge"], first]),
        "xs": lambda: act(T.xs[:], T.ge[:].indirect(T.tu[:, 10:16]), COPY, scale=STEP, after=[k["ge"], k["tc"], first]),
        "cg": lambda: v("cp", T.cg[:], T.cb[:, 16:112].indirect(T.tu[:, 10:16]), after=[k["c1"], k["tc"]]),
        "jz": lambda: act(T.jz[:], T.ramp[:, 0:8], scale=16.0 * U, bias=Q12, after=[q12]),
        "p96": lambda: v("ts", T.ti[:, 11:12], T.pc[:, 0:1], 96, op.bitwise_and),
        "tu8": lambda: v("cp", T.tu[:, 4:10], T.ti[:, 4:10]),
        "trl": trl, "counts1": counts1,
        "win0": lambda: [act(T.win1[:, c:c + n], T.val1[:, 0:n], COPY, scale=0.0, after=[val1]) for c, n in ((0, 192), (192, 192), (384, 16))][-1],
        "s4": lambda: v("scan", T.s4[:], T.yy[:, 32:97], T.yy[:, 0:65], 0.0, op.add, op.subtract, after=[k["trl"]]),
        "back": lambda: v("ts", BACK, T.ti[:, 11:12], -1.0, op.mult, 240.0, op.add, after=[k["p96"]]),
        "base": lambda: v("tr", T.bt[:], T.s4[:, 32:64], after=[k["s4"]]),
        "cand": lambda: v("tt", T.cand[:], T.bt[:].indirect(T.tu[:, 4:10]), T.cg[:], op.add, after=[k["base"], k["cg"], k["tu8"]]),
        "order": lambda: v("scan", T.sc[:], T.xs[:], T.cand[:], 0.0, op.max, op.min, after=[k["cand"], k["xs"]]),
        "rowl": lambda: v("tr", T.rowp[:, 0:32], T.bml[:], after=[k["bml"]]),
        "rowc": lambda: v("tr", T.rowp[:, 6:38], T.bmc[:], after=[k["counts1"], k["rowl"]]),
        "of1": lambda: v("ts", T.of1[:], T.sc[:, 4:96:8], -1.0, op.add, after=[k["order"]]),
        "win1": lambda: v("cp", T.win1[:].indirect(T.of1[:]), T.val1[:], after=[k["of1"], k["win0"], val1]),
        "counts": lambda: send([(r, T.rowp[:, 0:U], row) for r in order[:-1]], "sp", [k["rowc"]]),
        "x0": lambda: pack(0), "x1": lambda: pack(1),
    }
    for name in FIRST.split():
        k[name] = steps[name]()
    rowp, counts, win1, back, sc = k["rowc"], k["counts"], k["win1"], k["back"], k["order"]
    l_o = dma("y", row, T.rowp[:, 0:U], "d_o", after=[rowp])
    l_e3 = dma("y", T.e[:, 16:16 + U], T.lists[:], "d_e3", after=[lists])

    iota(T.tb2[:], [[0, 128]], 128, 0)
    tb0 = iota(T.tb0[:], [[0, N], [16, 5]], 128, 0)
    iota(T.z[:], [[0, 64]], 0, 0)
    iota(T.land[:, 0:16], [[0, 16]], 128, 0)
    t80 = iota(T.t80[:], [[SLOT, N + 1], [0, U]], -129 - SLOT, 0)
    side = act(SIDE, T.qf[:], FN.Sign, bias=0.5 - U)
    ja = act(T.ja[:], T.jz[:], scale=0.2 / U, bias=128.6 - 2.0 / U, after=[k["jz"]])
    for a in range(NB):
        rank = act(T.col[BLK[a], 1:2], T.col[BLK[a], 0:1], scale=(me - order[a]) / 2, bias=(me + order[a]) / 2, after=[side])
    jt = act(T.jt[:], T.ja[:], scale=0.2 - 5 * U, bias=129 * (5 * U - 0.2) - 0.4, after=[ja])
    nlt = act(NLT, T.rowp[:, me:me + 1], scale=-1.0, bias=-192.0, after=[rowp])

    def turn(i):
        for u in (0, 16):
            out, in_ = T.dup1[:, 5 * i:5 * i + 5, u:u + 16], T.win1[:, order[i]:400:5]
            t = v("cp", out, in_, after=[win1]) if i in (2, 3) else act(out, in_, COPY, after=[win1])
        if i == NB:
            k["tb2"] = act(T.tb2[:, 0:125:5], T.tb0[:], bias=T.qf[:], after=[tb0])
        return t

    def list1(step, i0, i1, after):
        if step == 0:
            return v("tr", T.tr1[:, 160 * i0:160 * i1], T.dup1[:, 5 * i0:5 * i1, :], after=after)
        if step == 1:
            return v("tt", T.sm1[:, 5 * i0:5 * i1], T.tr1[:, 160 * i0 + 8:160 * i1:32], T.tr1[:, 160 * i0 + 16:160 * i1:32], op.add, after=after)
        return v("ts", T.l1[:, 5 * i0:5 * i1], T.sm1[:, 5 * i0:5 * i1], BACK, op.add, after=after)

    def ge3():
        return v("tt", T.ea[:], T.e[:, 16:32].indirect(T.tu[:, 0:2]), T.thr[:, 16 * me:16 * me + 32], op.is_ge, after=[l_e3, t80])

    def l1c():
        t = list1(2, 4, 5, [k["sumc"], back])
        k["ownp1"] = planes(T.pl[:, cut(me, SLOT)], T.p, T.l1[:, 20:25], [t])
        return t

    def codes1(i):
        t = codes(T.q2[:, 160 * i:160 * i + 160], T.q, T.l1[:, 10 * i:10 * i + 10], [k["l1" + "ab"[i]], k["x2"]])
        return send([(order[j], u8(T.q2[:, cut(j, SENT1)]), u8(T.ql[:, cut(me, SENT1)])) for j in (2 * i, 2 * i + 1)], "s1c", [t])

    def planes1():
        for a in range(NB):
            own = act(T.z[BLK[a], U:U + 3], T.sc[BLK[a], 24 * a + 4:24 * a + 24:8], bias=T.col[BLK[a], 4:5], after=[nlt, sc, t80])
        planes(T.p2[:, 160:320], T.p, T.l1[:, 10:20], [k["l1b"], k["x2"]])
        k["own"] = act(T.z[:, 32 + U:35 + U], T.z[:, U:U + 3], COPY, after=[own])
        pa = planes(T.p2[:, 0:160], T.p, T.l1[:, 0:10], [k["l1a"]])
        k["ci0"] = act(T.ci0[:], T.land[:, 6:76], scale=0.2, bias=167.8 - 0.2 * me, after=[counts, l_o])
        k["kc"] = act(KC, RANK, scale=-128.0, bias=SLOT * (209 + me) - 200.6)
        return send([(r, T.p2[:, cut(j, SENT1)], T.pl[:, cut(me, SENT1)]) for j, r in enumerate(order[:-1])], "s1p", [pa])

    def u2():
        t = v("scan", T.u2[:], T.rst[:], T.d2[:], 0.0, op.mult, op.add, after=[k["d2"]])
        k["gx"] = act(T.gx2[:], T.u2[:], scale=-STEP, bias=STEP / 2, after=[t])
        return t

    def rows():
        return v("ms", T.win3[:, mine:mine + COLS], 0.0)

    def xo():
        t = v("tt", T.xo[:], T.land[:, 16 + me:76:6], T.sel[:], op.mult, after=[k["is"], k["below"], counts, l_o])
        k["k1"] = act(T.jk[:, 0:5], T.xo[:, 0:10:2], scale=0.0025, bias=(0.2 * (209 + me) - 0.4) / 5, accum_out=K1, after=[t])
        return act(T.jk[:, 5:15], T.xo[:], accum_out=K3)

    def l2():
        for a, b, d in ((0, rest, me + 1), (rest, N, 0)):
            if b > a:
                t = v("ts", T.l2[:, 5 * a:5 * b], T.ss2[:, 25 * d + 4:25 * (d + b - a):5], float(SLOT * (N - 1) + SENT1 - 1), op.min, after=[k["ss2"]])
        return t

    def planes2():
        need = [k["l2"], k["ownp1"], k["planes1"]]
        pb = planes(T.p3[:, 160:320], T.pl, T.l2[:, 10:20], need)
        pa = v("cp", T.p3[:, 0:160], T.pl[:].indirect(T.l2[:, 0:10]), after=need)
        k["ownp2"] = planes(T.pm[:, cut(0, SLOT)], T.pl, T.l2[:, 20:25])
        for c in (0, 96):
            full = act(T.rst8[:, c:c + 96], T.ones[0:32, 0:96], COPY)
        k["rst8"] = act(T.rst8[:, 0:192:8], T.ones[0:32, 0:24], COPY, scale=0.0, after=[full])
        return send([(r, T.p3[:, cut(j, SLOT)], T.pm[:, cut(j + 1, SLOT)]) for j, r in enumerate(order[:-1])], "s2p", [pa, pb])

    def codes2(i):
        t = codes(T.q3[:, 160 * i:160 * i + 160], T.ql, T.l2[:, 10 * i:10 * i + 10], [k["l2"], k["own1"], k["codes1a"]])
        return send([(order[j], u8(T.q3[:, cut(j, SLOT)]), u8(T.qm[:, cut(j + 1, SLOT)])) for j in (2 * i, 2 * i + 1)], ("s2a", "s2b")[i], [t])

    def v3():
        t = v("tt", T.v3[:], T.b3[:], T.tp3[:], op.add, after=[k["b3"], k["tp3"]])
        for h in range(2):
            k["val3"] = dma("y", T.val3[16 * h:128:32, :], T.v3[:, 16 * h:16 * h + 16], "d_v3", after=[t, k["val0"]])

    def wide():
        k["wide2"] = act(T.dup3[:, 12:24, 16:32], T.win3[:, mine + 192:mine + COLS], COPY, after=[k["win3"]])
        v("cp", T.dup3[:, :, 0:16], T.win3[:, mine:mine + COLS], after=[k["win3"]])
        return v("cp", T.dup3[:, 0:12, 16:32], T.win3[:, mine:mine + 192])

    def blocks():
        for r in range(8):
            out, in_ = T.su3[:, r:192:8], T.tr3[BLK[r // 2], 16 * (r % 2):768:32]
            k["su%d" % (r // 6)] = act(out, in_, COPY, after=[k["trw"]]) if r // 6 else v("cp", out, in_, after=[k["trw"]])

    def l3():
        for a in range(NB):
            t = v("ts", T.l3[BLK[a], :], T.sw3[:, 7:192:8], 200.0, op.add, after=[k["sum8"]])
        return t
    steps = {
        "jw": lambda: v("tt", T.jw[:], T.jz[:], T.jt[:], op.add, after=[jt]),
        "of2": lambda: v("cp", T.of2[:], T.jw[:], after=[k["jw"]]),
        "tra": lambda: list1(0, 0, 2, [k["turn1"]]), "suma": lambda: list1(1, 0, 2, [k["tra"]]), "l1a": lambda: list1(2, 0, 2, [k["suma"], back]),
        "trb": lambda: list1(0, 2, 4, [k["turn3"]]), "sumb": lambda: list1(1, 2, 4, [k["trb"]]), "l1b": lambda: list1(2, 2, 4, [k["sumb"], back]),
        "trc": lambda: list1(0, 4, 5, [k["turn4"]]), "sumc": lambda: list1(1, 4, 5, [k["trc"]]), "l1c": l1c,
        "planes1": planes1, "codes1a": lambda: codes1(0), "codes1b": lambda: codes1(1),
        "own1": lambda: codes(T.ql[:, cut(me, SLOT)], T.q, T.l1[:, 20:25], [k["l1c"]]),
        "d2": lambda: v("tt", T.d2[:], T.land[:, 0:76].indirect(T.of2[:]), T.tb2[:], op.subtract, after=[k["of2"], k["tb2"], t80, counts, l_o]),
        "u2": u2, "ci2": lambda: v("tt", T.ci2[:], T.ci0[:], T.t80[:, 2:72], op.add, after=[k["ci0"], t80]),
        "fx2": lambda: v("tt", T.fx2[:], T.ci2[:].indirect(T.of2[:]), T.u2[:], op.subtract, after=[k["u2"], k["ci2"]]),
        "ss2": lambda: v("scan", T.ss2[:], T.gx2[:, 0:125], T.fx2[:, 0:125], 0.0, op.max, op.min, after=[k["fx2"], k["gx"]]),
        "l2": l2, "planes2": planes2, "codes2a": lambda: codes2(0), "codes2b": lambda: codes2(1),
        "own2": lambda: codes(T.qm[:, cut(0, SLOT)], T.ql, T.l2[:, 20:25]),
        "is": lambda: v("ts", T.sel[:, 0:10:2], T.ramp[:, 0:N], RANK, op.is_equal, -float(SLOT), op.mult, after=[rank]),
        "below": lambda: v("ts", T.sel[:, 1:10:2], T.ramp[:, 0:N], RANK, op.is_lt, after=[rank]),
        "val0": lambda: v("ms", T.val3[:, 0:240], 0.0), "ge3": ge3, "rows": rows, "xo": xo, "v3": v3,
        "scan3": lambda: v("scan", T.z[:, 32:32 + U], T.ea[:, 0:U], T.ea[:, 16:16 + U], 0.0, op.add, op.subtract, after=[k["ge3"]]),
        "rest3": lambda: v("ts", T.z[:, 0:U], T.z[:, 32:32 + U], T.z[:, 31 + U:32 + U], op.subtract, after=[k["scan3"]]),
        "tr3": lambda: v("tr", T.yy[:, 32:96], T.z[:], after=[k["rest3"], k["own"]]),
        "m3": lambda: v("scan", T.m3[:], T.yy[:, 64:96], T.yy[:, 31:63], 0.0, op.add, op.subtract, after=[k["tr3"]]),
        "b3": lambda: v("ts", T.b3[:], T.m3[:], 0.2 - SLOT, op.mult, KC, op.add, after=[k["m3"], k["kc"]]),
        "a3": lambda: v("ts", T.a3[:], T.m3[:], -0.2, op.mult, K1, op.add, after=[k["m3"], k["k1"]]),
        "tp3": lambda: v("ts", T.tp3[:], T.a3[:], -5.0 * SLOT, op.mult, K3, op.add, after=[k["a3"], k["xo"]]),
        "of3": lambda: v("cp", T.of3[:, 0:15], T.e[:, 16:31], after=[l_e3]),
        "win3": lambda: v("cp", T.win3[:].indirect(T.of3[:, 0:15]), T.val3[:, 0:240], after=[k["of3"], k["val3"], k["rows"]]),
        "wide": wide, "trw": lambda: v("tr", T.tr3[:], T.dup3[:], after=[k["wide"], k["wide2"]]),
        "blocks": blocks,
        "sum8": lambda: v("scan", T.sw3[:], T.rst8[:], T.su3[:], 0.0, op.mult, op.add, after=[k["su0"], k["su1"], k["rst8"]]),
        "l3": l3, "x2": lambda: pack(2), "w0": lambda: pack_w(0), "w1": lambda: pack_w(1),
    }
    steps.update({"turn%d" % i: lambda i=i: turn(i) for i in range(N)})
    for name in ORDER.split():
        k[name] = steps[name]()

    res, copied = (T.rs0, T.rs1), []
    for b, c in enumerate((slice(0, 3 * SLOT), slice(3 * SLOT, N * SLOT))):
        wait("m", [k["w0"], k["w1"], k["own2"], k["ownp2"], k["planes2"], k["codes2" + "ab"[b]]])
        for o in range(2):
            bank = T.ps[:, 512 * (2 * b + o):512 * (2 * b + o) + c.stop - c.start]
            t = mark(g.tensor.matmul_mx(bank, T.wq[:, 128 * o:128 * o + 128], T.wp[:, 128 * o:128 * o + 128],
                                        T.qm[:, c], T.pm[:, c], True, True), "m", 1)
            copied.append(act(res[o][:, c], bank, COPY, after=[t]))
    for n, (q, o, a, b) in enumerate(PIECES):
        c = slice(COLS * o + 16 * a, COLS * o + 16 * b)
        pick, need = res[o][:].indirect(T.l3[:, a:b]), [copied[o], copied[2 + o], k["l3"]]
        t = act(T.ys[:, c], pick, COPY, after=need) if q == "a" else v("cp", T.ys[:, c], pick, after=need)
        if n < len(PIECES) - 1:
            stored = dma("y", T.y[:, c], T.ys[:, c], "st", after=[t])
        else:
            wait("a", [dma("a", T.y[:, c], T.ys[:, c], "st2", after=[t])])
    wait("y", [stored])
    wait("g", [(s, count[s]) for s in ("v", "a", "g", "loc")])
